import numpy as np
import ml_dtypes


def mxq(x, axis, fmt="e4m3"):
    dtype, down = {"e4m3": (ml_dtypes.float8_e4m3fn, 7), "e5m2": (ml_dtypes.float8_e5m2, 14)}[fmt]
    v = np.moveaxis(np.asarray(x, np.float32).astype(ml_dtypes.bfloat16).astype(np.float64), axis, -1)
    blocks = v.reshape(v.shape[:-1] + (-1, 32))
    amax = np.abs(blocks).max(-1, keepdims=True)
    byte = np.maximum(np.where(amax > 0, np.frexp(amax)[1] - 1 + 127, 0) - down, 1)
    scale = np.exp2(byte - 127.0)
    codes = (blocks / scale).astype(np.float32).astype(dtype).astype(np.float64)
    return np.moveaxis((codes * scale).reshape(v.shape), -1, axis)


WIDE = False


def mx_kscale(k):
    if not WIDE:
        return np.ones(k)
    levels = np.array([10, -10, 5, -5, 0])
    if k % 512:
        return np.exp2(np.random.permutation(np.resize(levels, k // 32))).repeat(32)
    a = np.empty((k // 512, 16))
    for p in range(k // 512):
        a[p, :8] = np.random.permutation(np.resize(levels, 8))
        for g in range(8):
            far = levels[np.abs(levels - a[p, g]) >= 10]
            a[p, g + 8] = far[np.random.randint(len(far))]
    return np.exp2(a.ravel()).repeat(32)


def f64(x):
    return np.asarray(x).astype(np.float64)


def striped(idx):
    return np.tile(idx.reshape(-1, 16).T, (8, 1)).astype(np.uint16)


def unstriped(offs):
    return offs[:16].T.reshape(-1).astype(np.int64)


E2M1 = np.array([0.0, 0.5, 1.0, 1.5, 2.0, 3.0, 4.0, 6.0, -0.0, -0.5, -1.0, -1.5, -2.0, -3.0, -4.0, -6.0])


def pack_weight(w, fmt):
    k, n = w.shape
    w = f64(np.asarray(w, np.float32).astype(ml_dtypes.bfloat16)).reshape(k // 32, 32, n)
    amax = np.abs(w).max(1)
    if fmt == "e4m3":
        byte = np.frexp(amax)[1] - 1 + 127 - 7
    else:
        mant, ex = np.frexp(amax / 6.0)
        byte = np.where(mant > 0.5, ex, ex - 1) + 127
    byte = np.clip(np.where(amax > 0, byte, 1), 1, 254)
    scaled = (w * np.exp2(127.0 - byte)[:, None, :]).reshape(k, n).astype(np.float32)
    by_word = np.ascontiguousarray(scaled.reshape(k // 512, 128, 4, n).transpose(0, 1, 3, 2))
    if fmt == "e4m3":
        words = by_word.astype(ml_dtypes.float8_e4m3fn).view(np.uint8)
    else:
        c = by_word.astype(ml_dtypes.float4_e2m1fn).view(np.uint8) & 0xF
        words = (c[..., 0::2] | (c[..., 1::2] << 4)).reshape(k // 512, 128, 2 * n)
    return np.ascontiguousarray(words), np.ascontiguousarray(byte.astype(np.uint8).reshape(k // 512, 16, n))


def unpack_weight(words, scales, fmt):
    g, _, n = scales.shape
    words = np.ascontiguousarray(words).reshape(g, 128, n, -1)
    if fmt == "e4m3":
        vals = words.view(ml_dtypes.float8_e4m3fn).astype(np.float64)
    else:
        nib = np.empty((g, 128, n, 4), np.uint8)
        nib[..., 0::2] = words & 0xF
        nib[..., 1::2] = words >> 4
        vals = E2M1[nib]
    vals = vals * np.repeat(np.exp2(scales.astype(np.float64) - 127.0), 8, axis=1)[..., None]
    return vals.transpose(0, 1, 3, 2).reshape(g * 512, n)


def gelu(v):
    return 0.5 * v * (1.0 + np.tanh(np.sqrt(2.0 / np.pi) * (v + 0.044715 * v**3)))


T, S, P, K, H, N = 4096, 1024, 512, 1024, 1024, 512

def setup_inputs():
    n = np.random.standard_normal
    s = mx_kscale(K)[:, None]
    u = mx_kscale(H)[:, None]
    tab_words, tab_scales = pack_weight(n((K, T)) * s, "e4m3")
    w4_words, w4_scales = pack_weight(0.5 * n((K, H)) / np.sqrt(K) / s, "e2m1")
    return {
        "tab_words": tab_words, "tab_scales": tab_scales,
        "offs": striped(np.random.permutation(T)[:S]),
        "pos1": striped(np.random.permutation(S)[:P]),
        "pos2": striped(np.random.permutation(S)[:P]),
        "pos3": striped(np.random.permutation(S)[:P]),
        "w4_words": w4_words, "w4_scales": w4_scales,
        "att": (0.8 + 0.1 * n(H)).astype(np.float32),
        "lim": (1.8 + 0.1 * n(H)).astype(np.float32),
        "gain": (np.exp(0.3 * n(H)) * u[:, 0]).astype(np.float32),
        "ws": (n((H, N)) / np.sqrt(H) / u).astype(np.float32),
    }

def reference(tab_words, tab_scales, offs, pos1, pos2, pos3, w4_words, w4_scales, att, lim, gain, ws):
    v = unpack_weight(tab_words, tab_scales, "e4m3")[:, unstriped(offs)]
    w4 = unpack_weight(w4_words, w4_scales, "e2m1")
    h = w4.T @ v
    loss = np.exp(h[:, unstriped(pos1)])
    attach = h[:, unstriped(pos2)] + f64(att)[:, None]
    limit = h[:, unstriped(pos3)] + f64(lim)[:, None]
    layered = np.minimum(np.maximum(loss, attach), limit)
    z = f64(gain)[:, None] * layered
    zq = mxq(z, 0, "e4m3")
    wq = mxq(f64(ws), 0, "e4m3")
    out = wq.T @ zq
    return out

@@ -1,0 +1,259 @@
+from contextlib import ExitStack
+
+import concourse.mybir as mybir
+
+T, S, PICKS, K, H, N = 4096, 1024, 512, 1024, 1024, 512
+FLOPS = 2 * K * H * S + 2 * H * N * PICKS
+
+F32 = mybir.dt.float32
+BF16 = mybir.dt.bfloat16
+I32 = mybir.dt.int32
+U32 = mybir.dt.uint32
+U16 = mybir.dt.uint16
+U8 = mybir.dt.uint8
+FP8X4 = mybir.dt.float8_e4m3fn_x4
+FP4X4 = mybir.dt.float4_e2m1fn_x4
+ALU = mybir.AluOpType
+ACT = mybir.ActivationFunctionType
+
+P = 128
+PACK = 4
+PASS = P * PACK
+BANK = 512
+WINDOW = 2048
+WINDOWS = 4
+SLICES = H // P
+
+
+def tile_list_wildfire_layer_cession_kernel(
+    tc, tab_words, tab_scales, offs, pos1, pos2, pos3, w4_words, w4_scales, att, lim, gain, ws, out
+):
+    nc = tc.nc
+    with ExitStack() as ctx:
+        held = ctx.enter_context(tc.tile_pool(name="held", bufs=1))
+        ring = ctx.enter_context(tc.tile_pool(name="ring", bufs=3))
+        one = ctx.enter_context(tc.tile_pool(name="one", bufs=1))
+        psum_h = ctx.enter_context(tc.psum_pool(name="psum_h", bufs=4))
+        psum_o = ctx.enter_context(tc.psum_pool(name="psum_o", bufs=1))
+
+        offs_t = held.tile([P, S // 16], U16, name="offs_t")
+        pos1_t = held.tile([P, PICKS // 16], U16, name="pos1_t")
+        pos2_t = held.tile([P, PICKS // 16], U16, name="pos2_t")
+        pos3_t = held.tile([P, PICKS // 16], U16, name="pos3_t")
+
+        tab_sc = held.tile([P, T // 4], I32, name="tab_sc", align_bytes=64)
+        nc.scalar.dma_start(out=tab_sc[0:32, :], in_=tab_scales.rearrange("a q n -> q a n").bitcast(I32))
+        w4_sc_raw = held.tile([P, H // 4], I32, name="w4_sc_raw", align_bytes=64)
+        nc.scalar.dma_start(out=w4_sc_raw[0:32, :], in_=w4_scales.rearrange("a q n -> q a n").bitcast(I32))
+        nc.sync.dma_start(offs_t[:], offs)
+        w4_view = w4_words.rearrange("a p n -> p a n").bitcast(I32)
+        w4_raw0 = held.tile([P, 2, H // 4], I32, name="w4_raw0", align_bytes=64)
+        nc.sync.dma_start(out=w4_raw0[:], in_=w4_view[:, :, 0 : H // 4])
+        tab_w = []
+        for a in range(2):
+            tile_a = one.tile([P, T], I32, name="tab_w%d" % a, tag="big%d" % a, align_bytes=64)
+            nc.sync.dma_start(out=tile_a[:], in_=tab_words[a].rearrange("p t i -> p (t i)").bitcast(I32))
+            tab_w.append(tile_a)
+        nc.sync.dma_start(pos1_t[:], pos1)
+        nc.sync.dma_start(pos2_t[:], pos2)
+        nc.sync.dma_start(pos3_t[:], pos3)
+        cols = []
+        for name, vec in (("att_t", att), ("lim_t", lim), ("gain_t", gain)):
+            col = held.tile([P, 2, PACK], F32, name=name)
+            nc.gpsimd.dma_start(out=col[:], in_=vec.rearrange("(b p t) -> p b t", p=P, t=PACK))
+            cols.append(col)
+        att_t, lim_t, gain_t = cols
+
+        for raw in (w4_sc_raw, tab_sc):
+            nc.vector.memset(raw[32:64, :], 0)
+            nc.vector.memset(raw[64:128, :], 0)
+        planes = held.tile([P, 2, (S + H) // 4], I32, name="planes", align_bytes=64)
+        nc.vector.memset(planes[:], 0)
+
+        zero = held.tile([P, 8], F32, name="zero")
+        nc.gpsimd.memset(zero[:], 0.0)
+        windows = []
+        for w in range(WINDOWS):
+            win = held.tile([P, WINDOW], F32, name="win%d" % w)
+            nc.scalar.activation(win[:, S:WINDOW], zero[:, 0:1].to_broadcast([P, WINDOW - S]), ACT.Exp)
+            windows.append(win)
+
+        rows = one.tile([P, S + H], U8, name="rows", tag="rows", align_bytes=64)
+        nc.vector.tensor_copy(
+            out=rows[:, S : S + H].rearrange("p (b t m) -> p b t m", b=2, t=PACK),
+            in_=w4_sc_raw[:].bitcast(U8).rearrange("p (b m t) -> p b t m", b=2, t=PACK),
+        )
+        v_sc_rows = held.tile([P, S], U8, name="v_sc_rows", align_bytes=64)
+        nc.vector.tensor_copy(v_sc_rows[:], tab_sc[:].bitcast(U8).indirect(offs_t[:]))
+        w4_codes = [held.tile([P, 2, H], U8, name="w4_codes%d" % b, align_bytes=64) for b in range(2)]
+
+        def order_columns(b, raw):
+            nc.vector.tensor_copy(
+                out=w4_codes[b][:].bitcast(U16).rearrange("p a (t m) -> p a t m", t=PACK),
+                in_=raw[:].bitcast(U16).rearrange("p a (m t) -> p a t m", t=PACK),
+            )
+
+        order_columns(0, w4_raw0)
+        nc.vector.tensor_copy(rows[:, 0:S].bitcast(I32), v_sc_rows[:].bitcast(I32))
+        for q in range(4):
+            nc.scalar.dma_start(out=planes[32 * q : 32 * q + 4, :, :], in_=rows[8 * q : 8 * q + 8, :].bitcast(I32))
+        w4_raw1 = one.tile([P, 2, H // 4], I32, name="w4_raw1", tag="rows", align_bytes=64)
+        nc.sync.dma_start(out=w4_raw1[:], in_=w4_view[:, :, H // 4 : H // 2])
+
+        v_codes = []
+        for a in range(2):
+            codes = held.tile([P, S], U32, name="v_codes%d" % a, align_bytes=64)
+            for half in range(2):
+                nc.vector.tensor_copy(
+                    codes[:, half * BANK : (half + 1) * BANK],
+                    tab_w[a][:].bitcast(U32).indirect(offs_t[:, half * 32 : (half + 1) * 32]),
+                )
+            v_codes.append(codes)
+        order_columns(1, w4_raw1)
+
+        ws_raw = one.tile([P, 2, PACK, N], F32, name="ws_raw", tag="big0", align_bytes=64)
+        for b in range(2):
+            nc.sync.dma_start(
+                out=ws_raw[:, b, :, :], in_=ws[b * PASS : (b + 1) * PASS, :].rearrange("(p t) n -> p t n", t=PACK)
+            )
+        ws_il = [held.tile([P, N, PACK], BF16, name="ws_il%d" % b, align_bytes=64) for b in range(2)]
+        ws_codes = [held.tile([P, N], U32, name="ws_codes%d" % b, align_bytes=64) for b in range(2)]
+        ws_sc = [held.tile([P, N], U8, name="ws_sc%d" % b, align_bytes=64) for b in range(2)]
+        z_planes = [held.tile([P, PACK, PICKS], BF16, name="z_planes%d" % b, align_bytes=64) for b in range(2)]
+        z_il = [held.tile([P, PICKS, PACK], BF16, name="z_il%d" % b, align_bytes=64) for b in range(2)]
+        z_codes = [held.tile([P, PICKS], U32, name="z_codes%d" % b, align_bytes=64) for b in range(2)]
+        z_sc = [held.tile([P, PICKS], U8, name="z_sc%d" % b, align_bytes=64) for b in range(2)]
+        HALF = PICKS // 2
+
+        def interleave(copy, dst, src, c0, c1):
+            copy(
+                dst[:, c0:c1, :].rearrange("p (c i) t -> p c t i", i=4),
+                src[:, :, c0:c1].rearrange("p t (c i) -> p c t i", i=4),
+            )
+
+        def quantize(codes, scales, il, c0, c1):
+            nc.vector.quantize_mx(
+                out=codes[:, c0:c1].bitcast(FP8X4),
+                scales=scales[:, c0:c1],
+                in_=il[:, c0:c1, :].rearrange("p n t -> p (n t)"),
+            )
+
+        def first_product(i):
+            win = windows[i % WINDOWS]
+            b, t = divmod(i, PACK)
+            for half in range(2):
+                bank = psum_h.tile([P, BANK], F32, name="h_bank")
+                for a in range(2):
+                    nc.tensor.matmul_mx(
+                        out=bank[:],
+                        lhsT=w4_codes[b][:, a, 2 * P * t : 2 * P * (t + 1)].bitcast(FP4X4),
+                        lhsT_scale=planes[:, a, :].bitcast(U8)[:, S + P * i : S + P * (i + 1)],
+                        rhs=v_codes[a][:, half * BANK : (half + 1) * BANK].bitcast(FP8X4),
+                        rhs_scale=planes[:, a, :].bitcast(U8)[:, half * BANK : (half + 1) * BANK],
+                        start=(a == 0),
+                        stop=(a == 1),
+                    )
+                nc.scalar.copy(win[:, half * BANK : (half + 1) * BANK], bank[:])
+
+        loss, attach, limit, lifted, layered = {}, {}, {}, {}, {}
+
+        def pick_loss(i):
+            loss[i] = ring.tile([P, PICKS], F32, name="loss")
+            nc.scalar.activation(loss[i][:], windows[i % WINDOWS][:].indirect(pos1_t[:]), ACT.Exp)
+
+        def pick_terms(i):
+            attach[i] = ring.tile([P, PICKS], F32, name="attach")
+            limit[i] = ring.tile([P, PICKS], F32, name="limit", bufs=4)
+            nc.vector.tensor_copy(attach[i][:], windows[i % WINDOWS][:, 0:S].indirect(pos2_t[:]))
+            nc.vector.tensor_copy(limit[i][:], windows[i % WINDOWS][:, 0:S].indirect(pos3_t[:]))
+
+        def lift(i):
+            b, t = divmod(i, PACK)
+            lifted[i] = ring.tile([P, PICKS], F32, name="lifted")
+            nc.vector.scalar_tensor_tensor(
+                lifted[i][:], attach[i][:], att_t[:, b, t : t + 1], loss[i][:], ALU.add, ALU.max
+            )
+
+        def cap(i, dst, c0, c1):
+            b, t = divmod(i, PACK)
+            layered[i] = dst
+            nc.vector.scalar_tensor_tensor(
+                dst[:, c0:c1], limit[i][:, c0:c1], lim_t[:, b, t : t + 1], lifted[i][:, c0:c1], ALU.add, ALU.min
+            )
+
+        def money(i):
+            b, t = divmod(i, PACK)
+            nc.scalar.activation(z_planes[b][:, t, :], layered[i], ACT.Copy, scale=gain_t[:, b, t : t + 1])
+
+        acc = {}
+
+        def second_product(b, half):
+            for j in range(N // P):
+                if b == 0 and half == 0:
+                    acc[j, half] = psum_o.tile([P, HALF], F32, name="acc%d" % j)
+                if b == 0 and half == 1:
+                    acc[j, half] = psum_h.tile([P, BANK], F32, name="h_bank")
+                nc.tensor.matmul_mx(
+                    out=acc[j, half][:, 0:HALF],
+                    lhsT=ws_codes[b][:, j * P : (j + 1) * P].bitcast(FP8X4),
+                    lhsT_scale=ws_sc[b][:, j * P : (j + 1) * P],
+                    rhs=z_codes[b][:, half * HALF : (half + 1) * HALF].bitcast(FP8X4),
+                    rhs_scale=z_sc[b][:, half * HALF : (half + 1) * HALF],
+                    start=(b == 0),
+                    stop=(b == 1),
+                )
+
+        def ws_piece(c):
+            b, quarter = divmod(c, 4)
+            interleave(nc.scalar.copy, ws_il[b], ws_raw[:, b, :, :], quarter * P, (quarter + 1) * P)
+
+        first_product(0)
+        first_product(1)
+        pick_terms(0)
+        pick_loss(0)
+        pick_terms(1)
+        lift(0)
+        last = SLICES - 1
+        for i in range(last):
+            if i + 2 < SLICES:
+                first_product(i + 2)
+            pick_loss(i + 1)
+            if i < 4:
+                ws_piece(2 * i)
+                ws_piece(2 * i + 1)
+            if i > 4:
+                interleave(nc.scalar.copy, z_il[0], z_planes[0], (i - 5) * HALF, (i - 4) * HALF)
+            if i >= 1:
+                money(i - 1)
+            if i + 2 < SLICES:
+                pick_terms(i + 2)
+            lift(i + 1)
+            if i == 3:
+                quantize(ws_codes[0], ws_sc[0], ws_il[0], 0, N)
+            if i == last - 1:
+                quantize(ws_codes[1], ws_sc[1], ws_il[1], 0, N)
+            lay = one.tile([P, 2, PICKS], F32, name="layered")
+            cap(i, lay[:, 0, :], 0, PICKS)
+        money(last - 1)
+        quantize(z_codes[0], z_sc[0], z_il[0], 0, PICKS)
+        for half in range(2):
+            second_product(0, half)
+        for half in range(2):
+            cap(last, lay[:, 1, :], half * HALF, (half + 1) * HALF)
+        for half in range(2):
+            cs = slice(half * HALF, (half + 1) * HALF)
+            nc.vector.tensor_scalar(
+                z_planes[1][:, PACK - 1, cs], lay[:, 1, cs], gain_t[:, 1, PACK - 1 : PACK], None, ALU.mult
+            )
+        interleave(nc.vector.tensor_copy, z_il[1], z_planes[1], 0, HALF)
+        interleave(nc.vector.tensor_copy, z_il[1], z_planes[1], HALF, HALF + 96)
+        interleave(nc.scalar.copy, z_il[1], z_planes[1], HALF + 96, PICKS)
+        for half in range(2):
+            quantize(z_codes[1], z_sc[1], z_il[1], half * HALF, (half + 1) * HALF)
+        for half in range(2):
+            second_product(1, half)
+            for j in range(N // P):
+                res = held.tile([P, HALF], F32, name="res%d%d" % (j, half))
+                copy = nc.scalar.copy if j % 2 == 0 else nc.vector.tensor_copy
+                copy(res[:], acc[j, half][:, 0:HALF])
+                nc.sync.dma_start(out=out[j * P : (j + 1) * P, half * HALF : (half + 1) * HALF], in_=res[:])

@@ -1,6 +1,7 @@
 from contextlib import ExitStack
 
 import concourse.mybir as mybir
+from concourse.masks import make_identity
 
 T, S, PICKS, K, H, N = 4096, 1024, 512, 1024, 1024, 512
 FLOPS = 2 * K * H * S + 2 * H * N * PICKS
@@ -45,40 +46,52 @@ def tile_list_wildfire_layer_cession_kernel(
         nc.scalar.dma_start(out=tab_sc[0:32, :], in_=tab_scales.rearrange("a q n -> q a n").bitcast(I32))
         w4_sc_raw = held.tile([P, H // 4], I32, name="w4_sc_raw", align_bytes=64)
         nc.scalar.dma_start(out=w4_sc_raw[0:32, :], in_=w4_scales.rearrange("a q n -> q a n").bitcast(I32))
-        nc.sync.dma_start(offs_t[:], offs)
         w4_view = w4_words.rearrange("a p n -> p a n").bitcast(I32)
         w4_raw0 = held.tile([P, 2, H // 4], I32, name="w4_raw0", align_bytes=64)
         nc.sync.dma_start(out=w4_raw0[:], in_=w4_view[:, :, 0 : H // 4])
+        nc.sync.dma_start(offs_t[:], offs)
+        nc.sync.dma_start(pos1_t[:], pos1)
+        nc.sync.dma_start(pos2_t[:], pos2)
+        nc.sync.dma_start(pos3_t[:], pos3)
         tab_w = []
         for a in range(2):
             tile_a = one.tile([P, T], I32, name="tab_w%d" % a, tag="big%d" % a, align_bytes=64)
             nc.sync.dma_start(out=tile_a[:], in_=tab_words[a].rearrange("p t i -> p (t i)").bitcast(I32))
             tab_w.append(tile_a)
-        nc.sync.dma_start(pos1_t[:], pos1)
-        nc.sync.dma_start(pos2_t[:], pos2)
-        nc.sync.dma_start(pos3_t[:], pos3)
-        cols = []
-        for name, vec in (("att_t", att), ("lim_t", lim), ("gain_t", gain)):
-            col = held.tile([P, 2, PACK], F32, name=name)
-            nc.gpsimd.dma_start(out=col[:], in_=vec.rearrange("(b p t) -> p b t", p=P, t=PACK))
-            cols.append(col)
-        att_t, lim_t, gain_t = cols
+        w4_raw1 = held.tile([P, 2, H // 4], I32, name="w4_raw1", align_bytes=64)
+        nc.sync.dma_start(out=w4_raw1[:], in_=w4_view[:, :, H // 4 : H // 2])
 
+        zero = held.tile([P, 8], F32, name="zero")
+        nc.vector.memset(zero[:], 0.0)
         for raw in (w4_sc_raw, tab_sc):
             nc.vector.memset(raw[32:64, :], 0)
             nc.vector.memset(raw[64:128, :], 0)
         planes = held.tile([P, 2, (S + H) // 4], I32, name="planes", align_bytes=64)
         nc.vector.memset(planes[:], 0)
 
-        zero = held.tile([P, 8], F32, name="zero")
-        nc.gpsimd.memset(zero[:], 0.0)
+        term_rows = held.tile([P, PASS], F32, name="term_rows")
+        nc.gpsimd.memset(term_rows[:], 0.0)
+        for v, vec in enumerate((att, lim, gain)):
+            nc.gpsimd.dma_start(out=term_rows[2 * v : 2 * v + 2, :], in_=vec.rearrange("(b k) -> b k", b=2))
+        ident = held.tile([P, P], F32, name="ident")
+        make_identity(nc, ident[:])
+        turned = psum_h.tile([P, BANK], F32, name="h_bank")
+        for t in range(PACK):
+            nc.tensor.transpose(turned[:, t * P : (t + 1) * P], term_rows[:, t:PASS:PACK], ident[:])
+        terms = held.tile([P, PACK, 6], F32, name="terms")
+        nc.scalar.copy(terms[:], turned[:].rearrange("p (t j) -> p t j", t=PACK)[:, :, 0:6])
+
+        def term(v, i):
+            b, t = divmod(i, PACK)
+            return terms[:, t, 2 * v + b : 2 * v + b + 1]
+
         windows = []
         for w in range(WINDOWS):
             win = held.tile([P, WINDOW], F32, name="win%d" % w)
             nc.scalar.activation(win[:, S:WINDOW], zero[:, 0:1].to_broadcast([P, WINDOW - S]), ACT.Exp)
             windows.append(win)
 
-        rows = one.tile([P, S + H], U8, name="rows", tag="rows", align_bytes=64)
+        rows = held.tile([P, S + H], U8, name="rows", align_bytes=64)
         nc.vector.tensor_copy(
             out=rows[:, S : S + H].rearrange("p (b t m) -> p b t m", b=2, t=PACK),
             in_=w4_sc_raw[:].bitcast(U8).rearrange("p (b m t) -> p b t m", b=2, t=PACK),
@@ -97,8 +110,6 @@ def tile_list_wildfire_layer_cession_kernel(
         nc.vector.tensor_copy(rows[:, 0:S].bitcast(I32), v_sc_rows[:].bitcast(I32))
         for q in range(4):
             nc.scalar.dma_start(out=planes[32 * q : 32 * q + 4, :, :], in_=rows[8 * q : 8 * q + 8, :].bitcast(I32))
-        w4_raw1 = one.tile([P, 2, H // 4], I32, name="w4_raw1", tag="rows", align_bytes=64)
-        nc.sync.dma_start(out=w4_raw1[:], in_=w4_view[:, :, H // 4 : H // 2])
 
         v_codes = []
         for a in range(2):
@@ -171,19 +182,19 @@ def tile_list_wildfire_layer_cession_kernel(
             b, t = divmod(i, PACK)
             lifted[i] = ring.tile([P, PICKS], F32, name="lifted")
             nc.vector.scalar_tensor_tensor(
-                lifted[i][:], attach[i][:], att_t[:, b, t : t + 1], loss[i][:], ALU.add, ALU.max
+                lifted[i][:], attach[i][:], term(0, i), loss[i][:], ALU.add, ALU.max
             )
 
         def cap(i, dst, c0, c1):
             b, t = divmod(i, PACK)
             layered[i] = dst
             nc.vector.scalar_tensor_tensor(
-                dst[:, c0:c1], limit[i][:, c0:c1], lim_t[:, b, t : t + 1], lifted[i][:, c0:c1], ALU.add, ALU.min
+                dst[:, c0:c1], limit[i][:, c0:c1], term(1, i), lifted[i][:, c0:c1], ALU.add, ALU.min
             )
 
         def money(i):
             b, t = divmod(i, PACK)
-            nc.scalar.activation(z_planes[b][:, t, :], layered[i], ACT.Copy, scale=gain_t[:, b, t : t + 1])
+            nc.scalar.activation(z_planes[b][:, t, :], layered[i], ACT.Copy, scale=term(2, i))
 
         acc = {}
 
@@ -205,7 +216,10 @@ def tile_list_wildfire_layer_cession_kernel(
 
         def ws_piece(c):
             b, quarter = divmod(c, 4)
-            interleave(nc.scalar.copy, ws_il[b], ws_raw[:, b, :, :], quarter * P, (quarter + 1) * P)
+            cs = slice(quarter * P, (quarter + 1) * P)
+            nc.gpsimd.tensor_scalar(
+                ws_il[b][:, cs, :], ws_raw[:, b, :, cs].rearrange("p t n -> p n t"), 1.0, 0.0, ALU.mult, ALU.add
+            )
 
         first_product(0)
         first_product(1)
@@ -243,7 +257,7 @@ def tile_list_wildfire_layer_cession_kernel(
         for half in range(2):
             cs = slice(half * HALF, (half + 1) * HALF)
             nc.vector.tensor_scalar(
-                z_planes[1][:, PACK - 1, cs], lay[:, 1, cs], gain_t[:, 1, PACK - 1 : PACK], None, ALU.mult
+                z_planes[1][:, PACK - 1, cs], lay[:, 1, cs], term(2, last), None, ALU.mult
             )
         interleave(nc.vector.tensor_copy, z_il[1], z_planes[1], 0, HALF)
         interleave(nc.vector.tensor_copy, z_il[1], z_planes[1], HALF, HALF + 96)

@@ -34,7 +34,7 @@ def tile_list_wildfire_layer_cession_kernel(
         held = ctx.enter_context(tc.tile_pool(name="held", bufs=1))
         ring = ctx.enter_context(tc.tile_pool(name="ring", bufs=3))
         one = ctx.enter_context(tc.tile_pool(name="one", bufs=1))
-        psum_h = ctx.enter_context(tc.psum_pool(name="psum_h", bufs=4))
+        psum_h = ctx.enter_context(tc.psum_pool(name="psum_h", bufs=2))
         psum_o = ctx.enter_context(tc.psum_pool(name="psum_o", bufs=1))
 
         offs_t = held.tile([P, S // 16], U16, name="offs_t")
@@ -42,24 +42,28 @@ def tile_list_wildfire_layer_cession_kernel(
         pos2_t = held.tile([P, PICKS // 16], U16, name="pos2_t")
         pos3_t = held.tile([P, PICKS // 16], U16, name="pos3_t")
 
-        tab_sc = held.tile([P, T // 4], I32, name="tab_sc", align_bytes=64)
-        nc.scalar.dma_start(out=tab_sc[0:32, :], in_=tab_scales.rearrange("a q n -> q a n").bitcast(I32))
         w4_sc_raw = held.tile([P, H // 4], I32, name="w4_sc_raw", align_bytes=64)
         nc.scalar.dma_start(out=w4_sc_raw[0:32, :], in_=w4_scales.rearrange("a q n -> q a n").bitcast(I32))
+        tab_sc = held.tile([P, T // 4], I32, name="tab_sc", align_bytes=64)
+        nc.scalar.dma_start(out=tab_sc[0:32, :], in_=tab_scales.rearrange("a q n -> q a n").bitcast(I32))
         w4_view = w4_words.rearrange("a p n -> p a n").bitcast(I32)
         w4_raw0 = held.tile([P, 2, H // 4], I32, name="w4_raw0", align_bytes=64)
         nc.sync.dma_start(out=w4_raw0[:], in_=w4_view[:, :, 0 : H // 4])
         nc.sync.dma_start(offs_t[:], offs)
         nc.sync.dma_start(pos1_t[:], pos1)
-        nc.sync.dma_start(pos2_t[:], pos2)
-        nc.sync.dma_start(pos3_t[:], pos3)
         tab_w = []
-        for a in range(2):
+
+        def load_table(a):
             tile_a = one.tile([P, T], I32, name="tab_w%d" % a, tag="big%d" % a, align_bytes=64)
             nc.sync.dma_start(out=tile_a[:], in_=tab_words[a].rearrange("p t i -> p (t i)").bitcast(I32))
             tab_w.append(tile_a)
+
+        load_table(0)
+        load_table(1)
         w4_raw1 = held.tile([P, 2, H // 4], I32, name="w4_raw1", align_bytes=64)
         nc.sync.dma_start(out=w4_raw1[:], in_=w4_view[:, :, H // 4 : H // 2])
+        nc.sync.dma_start(pos2_t[:], pos2)
+        nc.sync.dma_start(pos3_t[:], pos3)
 
         zero = held.tile([P, 8], F32, name="zero")
         nc.vector.memset(zero[:], 0.0)
@@ -67,7 +71,7 @@ def tile_list_wildfire_layer_cession_kernel(
             nc.vector.memset(raw[32:64, :], 0)
             nc.vector.memset(raw[64:128, :], 0)
         planes = held.tile([P, 2, (S + H) // 4], I32, name="planes", align_bytes=64)
-        nc.vector.memset(planes[:], 0)
+        nc.gpsimd.memset(planes[:], 0)
 
         term_rows = held.tile([P, PASS], F32, name="term_rows")
         nc.gpsimd.memset(term_rows[:], 0.0)
@@ -75,11 +79,7 @@ def tile_list_wildfire_layer_cession_kernel(
             nc.gpsimd.dma_start(out=term_rows[2 * v : 2 * v + 2, :], in_=vec.rearrange("(b k) -> b k", b=2))
         ident = held.tile([P, P], F32, name="ident")
         make_identity(nc, ident[:])
-        turned = psum_h.tile([P, BANK], F32, name="h_bank")
-        for t in range(PACK):
-            nc.tensor.transpose(turned[:, t * P : (t + 1) * P], term_rows[:, t:PASS:PACK], ident[:])
         terms = held.tile([P, PACK, 6], F32, name="terms")
-        nc.scalar.copy(terms[:], turned[:].rearrange("p (t j) -> p t j", t=PACK)[:, :, 0:6])
 
         def term(v, i):
             b, t = divmod(i, PACK)
@@ -106,10 +106,10 @@ def tile_list_wildfire_layer_cession_kernel(
                 in_=raw[:].bitcast(U16).rearrange("p a (m t) -> p a t m", t=PACK),
             )
 
-        order_columns(0, w4_raw0)
         nc.vector.tensor_copy(rows[:, 0:S].bitcast(I32), v_sc_rows[:].bitcast(I32))
         for q in range(4):
             nc.scalar.dma_start(out=planes[32 * q : 32 * q + 4, :, :], in_=rows[8 * q : 8 * q + 8, :].bitcast(I32))
+        order_columns(0, w4_raw0)
 
         v_codes = []
         for a in range(2):
@@ -131,78 +131,78 @@ def tile_list_wildfire_layer_cession_kernel(
         ws_codes = [held.tile([P, N], U32, name="ws_codes%d" % b, align_bytes=64) for b in range(2)]
         ws_sc = [held.tile([P, N], U8, name="ws_sc%d" % b, align_bytes=64) for b in range(2)]
         z_planes = [held.tile([P, PACK, PICKS], BF16, name="z_planes%d" % b, align_bytes=64) for b in range(2)]
-        z_il = [held.tile([P, PICKS, PACK], BF16, name="z_il%d" % b, align_bytes=64) for b in range(2)]
+        HALF = PICKS // 2
+        z_il0 = held.tile([P, PICKS, PACK], BF16, name="z_il0", align_bytes=64)
         z_codes = [held.tile([P, PICKS], U32, name="z_codes%d" % b, align_bytes=64) for b in range(2)]
         z_sc = [held.tile([P, PICKS], U8, name="z_sc%d" % b, align_bytes=64) for b in range(2)]
-        HALF = PICKS // 2
 
-        def interleave(copy, dst, src, c0, c1):
-            copy(
-                dst[:, c0:c1, :].rearrange("p (c i) t -> p c t i", i=4),
-                src[:, :, c0:c1].rearrange("p t (c i) -> p c t i", i=4),
+        def interleave(copy, dst, src):
+            copy(dst.rearrange("p (c i) t -> p c t i", i=4), src.rearrange("p t (c i) -> p c t i", i=4))
+
+        def quantize(codes, scales, il):
+            nc.vector.quantize_mx(out=codes.bitcast(FP8X4), scales=scales, in_=il.rearrange("p n t -> p (n t)"))
+
+        def h_pass(i, a, dst, c0, c1, start, stop):
+            b, t = divmod(i, PACK)
+            nc.tensor.matmul_mx(
+                out=dst,
+                lhsT=w4_codes[b][:, a, 2 * P * t : 2 * P * (t + 1)].bitcast(FP4X4),
+                lhsT_scale=planes[:, a, :].bitcast(U8)[:, S + P * i : S + P * (i + 1)],
+                rhs=v_codes[a][:, c0:c1].bitcast(FP8X4),
+                rhs_scale=planes[:, a, :].bitcast(U8)[:, c0:c1],
+                start=start,
+                stop=stop,
             )
 
-        def quantize(codes, scales, il, c0, c1):
-            nc.vector.quantize_mx(
-                out=codes[:, c0:c1].bitcast(FP8X4),
-                scales=scales[:, c0:c1],
-                in_=il[:, c0:c1, :].rearrange("p n t -> p (n t)"),
-            )
+        def h_bank(i, half):
+            bank = psum_h.tile([P, BANK], F32, name="h_bank")
+            for a in range(2):
+                h_pass(i, a, bank[:], half * BANK, (half + 1) * BANK, a == 0, a == 1)
+            nc.scalar.copy(windows[i % WINDOWS][:, half * BANK : (half + 1) * BANK], bank[:])
 
         def first_product(i):
-            win = windows[i % WINDOWS]
-            b, t = divmod(i, PACK)
             for half in range(2):
-                bank = psum_h.tile([P, BANK], F32, name="h_bank")
-                for a in range(2):
-                    nc.tensor.matmul_mx(
-                        out=bank[:],
-                        lhsT=w4_codes[b][:, a, 2 * P * t : 2 * P * (t + 1)].bitcast(FP4X4),
-                        lhsT_scale=planes[:, a, :].bitcast(U8)[:, S + P * i : S + P * (i + 1)],
-                        rhs=v_codes[a][:, half * BANK : (half + 1) * BANK].bitcast(FP8X4),
-                        rhs_scale=planes[:, a, :].bitcast(U8)[:, half * BANK : (half + 1) * BANK],
-                        start=(a == 0),
-                        stop=(a == 1),
-                    )
-                nc.scalar.copy(win[:, half * BANK : (half + 1) * BANK], bank[:])
+                h_bank(i, half)
 
-        loss, attach, limit, lifted, layered = {}, {}, {}, {}, {}
+        def first_slice():
+            h_bank(0, 0)
+            for q, copy in enumerate((nc.scalar.copy, nc.vector.tensor_copy)):
+                bank = psum_o.tile([P, HALF], F32, name="acc%d0" % q)
+                c0 = BANK + q * HALF
+                for a in range(2):
+                    for u in range(2):
+                        h_pass(
+                            0, a, bank[:, u * P : (u + 1) * P], c0 + u * P, c0 + (u + 1) * P,
+                            a == 0 and u == 0, a == 1 and u == 1,
+                        )
+                copy(windows[0][:, c0 : c0 + HALF], bank[:])
+
+        loss = {}
 
         def pick_loss(i):
             loss[i] = ring.tile([P, PICKS], F32, name="loss")
             nc.scalar.activation(loss[i][:], windows[i % WINDOWS][:].indirect(pos1_t[:]), ACT.Exp)
 
-        def pick_terms(i):
-            attach[i] = ring.tile([P, PICKS], F32, name="attach")
-            limit[i] = ring.tile([P, PICKS], F32, name="limit", bufs=4)
-            nc.vector.tensor_copy(attach[i][:], windows[i % WINDOWS][:, 0:S].indirect(pos2_t[:]))
-            nc.vector.tensor_copy(limit[i][:], windows[i % WINDOWS][:, 0:S].indirect(pos3_t[:]))
+        def pick(dst, i, pos_t, c0, c1):
+            nc.vector.tensor_copy(dst, windows[i % WINDOWS][:, 0:S].indirect(pos_t[:, c0 // 16 : c1 // 16]))
 
-        def lift(i):
-            b, t = divmod(i, PACK)
-            lifted[i] = ring.tile([P, PICKS], F32, name="lifted")
-            nc.vector.scalar_tensor_tensor(
-                lifted[i][:], attach[i][:], term(0, i), loss[i][:], ALU.add, ALU.max
-            )
+        def lift(dst, i, attach, c0, c1):
+            nc.vector.scalar_tensor_tensor(dst, attach, term(0, i), loss[i][:, c0:c1], ALU.add, ALU.max)
 
-        def cap(i, dst, c0, c1):
-            b, t = divmod(i, PACK)
-            layered[i] = dst
-            nc.vector.scalar_tensor_tensor(
-                dst[:, c0:c1], limit[i][:, c0:c1], term(1, i), lifted[i][:, c0:c1], ALU.add, ALU.min
-            )
+        def cap(dst, i, limit, lifted):
+            nc.vector.scalar_tensor_tensor(dst, limit, term(1, i), lifted, ALU.add, ALU.min)
 
-        def money(i):
+        def money(i, layered, c0, c1):
             b, t = divmod(i, PACK)
-            nc.scalar.activation(z_planes[b][:, t, :], layered[i], ACT.Copy, scale=term(2, i))
+            nc.scalar.activation(z_planes[b][:, t, c0:c1], layered, ACT.Copy, scale=term(2, i))
 
         acc = {}
 
         def second_product(b, half):
             for j in range(N // P):
-                if b == 0 and half == 0:
-                    acc[j, half] = psum_o.tile([P, HALF], F32, name="acc%d" % j)
-                if b == 0 and half == 1:
+                if b == 0 and (half == 0 or j < 2):
+                    acc[j, half] = psum_o.tile([P, HALF], F32, name="acc%d%d" % (j, half))
+                elif b == 0:
                     acc[j, half] = psum_h.tile([P, BANK], F32, name="h_bank")
                 nc.tensor.matmul_mx(
                     out=acc[j, half][:, 0:HALF],
@@ -214,60 +214,81 @@ def tile_list_wildfire_layer_cession_kernel(
                     stop=(b == 1),
                 )
 
-        def ws_piece(c):
-            b, quarter = divmod(c, 4)
+        def store(half, copies):
+            for j in range(N // P):
+                res = held.tile([P, HALF], F32, name="res%d%d" % (j, half))
+                copies[j % 2](res[:], acc[j, half][:, 0:HALF])
+                nc.sync.dma_start(out=out[j * P : (j + 1) * P, half * HALF : (half + 1) * HALF], in_=res[:])
+
+        for quarter in range(4):
             cs = slice(quarter * P, (quarter + 1) * P)
             nc.gpsimd.tensor_scalar(
-                ws_il[b][:, cs, :], ws_raw[:, b, :, cs].rearrange("p t n -> p n t"), 1.0, 0.0, ALU.mult, ALU.add
+                ws_il[0][:, cs, :], ws_raw[:, 0, :, cs].rearrange("p t n -> p n t"), 1.0, 0.0, ALU.mult, ALU.add
             )
 
-        first_product(0)
+        first_slice()
         first_product(1)
+        turned = psum_h.tile([P, BANK], F32, name="h_bank")
+        for t in range(PACK):
+            nc.tensor.transpose(turned[:, t * P : (t + 1) * P], term_rows[:, t:PASS:PACK], ident[:])
+        nc.scalar.copy(terms[:], turned[:].rearrange("p (t j) -> p t j", t=PACK)[:, :, 0:6])
+
+
+        attach, limit, lifted, layered = {}, {}, {}, {}
+
+        def pick_terms(i):
+            attach[i] = ring.tile([P, PICKS], F32, name="attach")
+            limit[i] = ring.tile([P, PICKS], F32, name="limit", bufs=4)
+            pick(attach[i][:], i, pos2_t, 0, PICKS)
+            pick(limit[i][:], i, pos3_t, 0, PICKS)
+
+        def lift_whole(i):
+            lifted[i] = ring.tile([P, PICKS], F32, name="lifted")
+            lift(lifted[i][:], i, attach[i][:], 0, PICKS)
+
         pick_terms(0)
         pick_loss(0)
         pick_terms(1)
-        lift(0)
+        lift_whole(0)
         last = SLICES - 1
         for i in range(last):
             if i + 2 < SLICES:
                 first_product(i + 2)
             pick_loss(i + 1)
             if i < 4:
-                ws_piece(2 * i)
-                ws_piece(2 * i + 1)
+                cs = slice(i * P, (i + 1) * P)
+                interleave(nc.scalar.copy, ws_il[1][:, cs, :], ws_raw[:, 1, :, cs])
             if i > 4:
-                interleave(nc.scalar.copy, z_il[0], z_planes[0], (i - 5) * HALF, (i - 4) * HALF)
+                cs = slice((i - 5) * HALF, (i - 4) * HALF)
+                interleave(nc.scalar.copy, z_il0[:, cs, :], z_planes[0][:, :, cs])
             if i >= 1:
-                money(i - 1)
+                money(i - 1, layered[i - 1], 0, PICKS)
             if i + 2 < SLICES:
                 pick_terms(i + 2)
-            lift(i + 1)
-            if i == 3:
-                quantize(ws_codes[0], ws_sc[0], ws_il[0], 0, N)
-            if i == last - 1:
-                quantize(ws_codes[1], ws_sc[1], ws_il[1], 0, N)
+            lift_whole(i + 1)
+            if i == 1:
+                quantize(ws_codes[0][:], ws_sc[0][:], ws_il[0][:])
+            if i == 4:
+                quantize(ws_codes[1][:], ws_sc[1][:], ws_il[1][:])
             lay = one.tile([P, 2, PICKS], F32, name="layered")
-            cap(i, lay[:, 0, :], 0, PICKS)
-        money(last - 1)
-        quantize(z_codes[0], z_sc[0], z_il[0], 0, PICKS)
+            layered[i] = lay[:, 0, :]
+            cap(layered[i], i, limit[i][:], lifted[i][:])
+        money(last - 1, layered[last - 1], 0, PICKS)
+        quantize(z_codes[0][:], z_sc[0][:], z_il0[:])
         for half in range(2):
             second_product(0, half)
-        for half in range(2):
-            cap(last, lay[:, 1, :], half * HALF, (half + 1) * HALF)
-        for half in range(2):
-            cs = slice(half * HALF, (half + 1) * HALF)
-            nc.vector.tensor_scalar(
-                z_planes[1][:, PACK - 1, cs], lay[:, 1, cs], term(2, last), None, ALU.mult
-            )
-        interleave(nc.vector.tensor_copy, z_il[1], z_planes[1], 0, HALF)
-        interleave(nc.vector.tensor_copy, z_il[1], z_planes[1], HALF, HALF + 96)
-        interleave(nc.scalar.copy, z_il[1], z_planes[1], HALF + 96, PICKS)
-        for half in range(2):
-            quantize(z_codes[1], z_sc[1], z_il[1], half * HALF, (half + 1) * HALF)
+        halves = [slice(half * HALF, (half + 1) * HALF) for half in range(2)]
+        for cs in halves:
+            cap(lay[:, 1, cs], last, limit[last][:, cs], lifted[last][:, cs])
+        for cs in halves:
+            nc.vector.tensor_scalar(z_planes[1][:, PACK - 1, cs], lay[:, 1, cs], term(2, last), None, ALU.mult)
+        z_il1 = held.tile([P, PICKS, PACK], BF16, name="z_il1", align_bytes=64)
+        SHARE = HALF + 96
+        interleave(nc.vector.tensor_copy, z_il1[:, 0:HALF, :], z_planes[1][:, :, 0:HALF])
+        interleave(nc.vector.tensor_copy, z_il1[:, HALF:SHARE, :], z_planes[1][:, :, HALF:SHARE])
+        interleave(nc.scalar.copy, z_il1[:, SHARE:PICKS, :], z_planes[1][:, :, SHARE:PICKS])
+        for cs in halves:
+            quantize(z_codes[1][:, cs], z_sc[1][:, cs], z_il1[:, cs, :])
         for half in range(2):
             second_product(1, half)
-            for j in range(N // P):
-                res = held.tile([P, HALF], F32, name="res%d%d" % (j, half))
-                copy = nc.scalar.copy if j % 2 == 0 else nc.vector.tensor_copy
-                copy(res[:], acc[j, half][:, 0:HALF])
-                nc.sync.dma_start(out=out[j * P : (j + 1) * P, half * HALF : (half + 1) * HALF], in_=res[:])
+            store(half, (nc.scalar.copy, nc.vector.tensor_copy))

@@ -43,25 +43,22 @@ def tile_list_wildfire_layer_cession_kernel(
         pos3_t = held.tile([P, PICKS // 16], U16, name="pos3_t")
 
         w4_sc_raw = held.tile([P, H // 4], I32, name="w4_sc_raw", align_bytes=64)
-        nc.scalar.dma_start(out=w4_sc_raw[0:32, :], in_=w4_scales.rearrange("a q n -> q a n").bitcast(I32))
         tab_sc = held.tile([P, T // 4], I32, name="tab_sc", align_bytes=64)
-        nc.scalar.dma_start(out=tab_sc[0:32, :], in_=tab_scales.rearrange("a q n -> q a n").bitcast(I32))
+        for raw, scales in ((tab_sc, tab_scales), (w4_sc_raw, w4_scales)):
+            for a in range(2):
+                nc.sync.dma_start(
+                    out=raw[a:32:2, :], in_=scales[a].rearrange("(u r) n -> r u n", r=4).bitcast(I32)
+                )
         w4_view = w4_words.rearrange("a p n -> p a n").bitcast(I32)
         w4_raw0 = held.tile([P, 2, H // 4], I32, name="w4_raw0", align_bytes=64)
-        nc.sync.dma_start(out=w4_raw0[:], in_=w4_view[:, :, 0 : H // 4])
         nc.sync.dma_start(offs_t[:], offs)
-        nc.sync.dma_start(pos1_t[:], pos1)
+        nc.sync.dma_start(out=w4_raw0[:], in_=w4_view[:, :, 0 : H // 4])
         tab_w = []
-
-        def load_table(a):
+        for a in range(2):
             tile_a = one.tile([P, T], I32, name="tab_w%d" % a, tag="big%d" % a, align_bytes=64)
             nc.sync.dma_start(out=tile_a[:], in_=tab_words[a].rearrange("p t i -> p (t i)").bitcast(I32))
             tab_w.append(tile_a)
-
-        load_table(0)
-        load_table(1)
-        w4_raw1 = held.tile([P, 2, H // 4], I32, name="w4_raw1", align_bytes=64)
-        nc.sync.dma_start(out=w4_raw1[:], in_=w4_view[:, :, H // 4 : H // 2])
+        nc.sync.dma_start(pos1_t[:], pos1)
         nc.sync.dma_start(pos2_t[:], pos2)
         nc.sync.dma_start(pos3_t[:], pos3)
 
@@ -70,15 +67,19 @@ def tile_list_wildfire_layer_cession_kernel(
         for raw in (w4_sc_raw, tab_sc):
             nc.vector.memset(raw[32:64, :], 0)
             nc.vector.memset(raw[64:128, :], 0)
-        planes = held.tile([P, 2, (S + H) // 4], I32, name="planes", align_bytes=64)
-        nc.gpsimd.memset(planes[:], 0)
+        EARLY = S + PASS
+        planes_early = held.tile([P, 2, EARLY // 4], I32, name="planes_early", align_bytes=64)
+        planes_late = held.tile([P, 2, PASS // 4], I32, name="planes_late", align_bytes=64)
+        nc.gpsimd.memset(planes_early[:], 0)
+        nc.gpsimd.memset(planes_late[:], 0)
 
-        term_rows = held.tile([P, PASS], F32, name="term_rows")
-        nc.gpsimd.memset(term_rows[:], 0.0)
+        term_raw = held.tile([P, PASS], F32, name="term_raw")
+        nc.gpsimd.memset(term_raw[:], 0.0)
         for v, vec in enumerate((att, lim, gain)):
-            nc.gpsimd.dma_start(out=term_rows[2 * v : 2 * v + 2, :], in_=vec.rearrange("(b k) -> b k", b=2))
+            nc.gpsimd.dma_start(out=term_raw[2 * v : 2 * v + 2, :], in_=vec.rearrange("(b k) -> b k", b=2))
         ident = held.tile([P, P], F32, name="ident")
         make_identity(nc, ident[:])
+        term_rows = held.tile([P, PACK, P], F32, name="term_rows")
         terms = held.tile([P, PACK, 6], F32, name="terms")
 
         def term(v, i):
@@ -87,28 +88,36 @@ def tile_list_wildfire_layer_cession_kernel(
 
         windows = []
         for w in range(WINDOWS):
-            win = held.tile([P, WINDOW], F32, name="win%d" % w)
+            win = held.tile([P, WINDOW], F32, name="win%d" % w, align_bytes=64)
             nc.scalar.activation(win[:, S:WINDOW], zero[:, 0:1].to_broadcast([P, WINDOW - S]), ACT.Exp)
             windows.append(win)
 
-        rows = held.tile([P, S + H], U8, name="rows", align_bytes=64)
-        nc.vector.tensor_copy(
-            out=rows[:, S : S + H].rearrange("p (b t m) -> p b t m", b=2, t=PACK),
-            in_=w4_sc_raw[:].bitcast(U8).rearrange("p (b m t) -> p b t m", b=2, t=PACK),
+        nc.scalar.copy(
+            term_rows[:].rearrange("p t (g q) -> p t g q", q=8), term_raw[:].rearrange("p (g t q) -> p t g q", t=PACK, q=8)
         )
-        v_sc_rows = held.tile([P, S], U8, name="v_sc_rows", align_bytes=64)
+
+        rows = held.tile([P, (S + H) // 4], I32, name="rows", align_bytes=64)
+        nc.vector.tensor_copy(
+            out=rows[:, S // 4 :].rearrange("p (b t g k) -> p b t g k", b=2, t=PACK, k=2),
+            in_=w4_sc_raw[:].rearrange("p (b g t k) -> p b t g k", b=2, t=PACK, k=2),
+        )
+        v_sc_rows = one.tile([P, S], U8, name="v_sc_rows", tag="late", align_bytes=64)
         nc.vector.tensor_copy(v_sc_rows[:], tab_sc[:].bitcast(U8).indirect(offs_t[:]))
-        w4_codes = [held.tile([P, 2, H], U8, name="w4_codes%d" % b, align_bytes=64) for b in range(2)]
+        w4_codes = [held.tile([P, 2, H // 4], I32, name="w4_codes%d" % b, align_bytes=64) for b in range(2)]
 
         def order_columns(b, raw):
             nc.vector.tensor_copy(
-                out=w4_codes[b][:].bitcast(U16).rearrange("p a (t m) -> p a t m", t=PACK),
-                in_=raw[:].bitcast(U16).rearrange("p a (m t) -> p a t m", t=PACK),
+                out=w4_codes[b][:].rearrange("p a (t g k) -> p a t g k", t=PACK, k=4),
+                in_=raw[:].rearrange("p a (g t k) -> p a t g k", t=PACK, k=4),
             )
 
-        nc.vector.tensor_copy(rows[:, 0:S].bitcast(I32), v_sc_rows[:].bitcast(I32))
+        nc.vector.tensor_copy(rows[:, 0 : S // 4], v_sc_rows[:].bitcast(I32))
         for q in range(4):
-            nc.scalar.dma_start(out=planes[32 * q : 32 * q + 4, :, :], in_=rows[8 * q : 8 * q + 8, :].bitcast(I32))
+            nc.sync.dma_start(out=planes_early[q:P:32, :, :], in_=rows[8 * q : 8 * q + 8, 0 : EARLY // 4])
+        w4_raw1 = one.tile([P, 2, H // 4], I32, name="w4_raw1", tag="late", align_bytes=64)
+        nc.sync.dma_start(out=w4_raw1[:], in_=w4_view[:, :, H // 4 : H // 2])
+        for q in range(4):
+            nc.sync.dma_start(out=planes_late[q:P:32, :, :], in_=rows[8 * q : 8 * q + 8, EARLY // 4 :])
         order_columns(0, w4_raw0)
 
         v_codes = []
@@ -123,10 +132,10 @@ def tile_list_wildfire_layer_cession_kernel(
         order_columns(1, w4_raw1)
 
         ws_raw = one.tile([P, 2, PACK, N], F32, name="ws_raw", tag="big0", align_bytes=64)
+        ws_view = ws.rearrange("(b g t q) n -> b t g q n", b=2, t=PACK, q=8)
         for b in range(2):
-            nc.sync.dma_start(
-                out=ws_raw[:, b, :, :], in_=ws[b * PASS : (b + 1) * PASS, :].rearrange("(p t) n -> p t n", t=PACK)
-            )
+            for t in range(PACK):
+                nc.sync.dma_start(out=ws_raw[:, b, t, :], in_=ws_view[b, t])
         ws_il = [held.tile([P, N, PACK], BF16, name="ws_il%d" % b, align_bytes=64) for b in range(2)]
         ws_codes = [held.tile([P, N], U32, name="ws_codes%d" % b, align_bytes=64) for b in range(2)]
         ws_sc = [held.tile([P, N], U8, name="ws_sc%d" % b, align_bytes=64) for b in range(2)]
@@ -144,12 +153,16 @@ def tile_list_wildfire_layer_cession_kernel(
 
         def h_pass(i, a, dst, c0, c1, start, stop):
             b, t = divmod(i, PACK)
+            if b == 0:
+                w4_plane = planes_early[:, a, :].bitcast(U8)[:, S + P * t : S + P * (t + 1)]
+            else:
+                w4_plane = planes_late[:, a, :].bitcast(U8)[:, P * t : P * (t + 1)]
             nc.tensor.matmul_mx(
                 out=dst,
-                lhsT=w4_codes[b][:, a, 2 * P * t : 2 * P * (t + 1)].bitcast(FP4X4),
-                lhsT_scale=planes[:, a, :].bitcast(U8)[:, S + P * i : S + P * (i + 1)],
+                lhsT=w4_codes[b][:, a, :].bitcast(U8)[:, 2 * P * t : 2 * P * (t + 1)].bitcast(FP4X4),
+                lhsT_scale=w4_plane,
                 rhs=v_codes[a][:, c0:c1].bitcast(FP8X4),
-                rhs_scale=planes[:, a, :].bitcast(U8)[:, c0:c1],
+                rhs_scale=planes_early[:, a, :].bitcast(U8)[:, c0:c1],
                 start=start,
                 stop=stop,
             )
@@ -165,17 +178,19 @@ def tile_list_wildfire_layer_cession_kernel(
                 h_bank(i, half)
 
         def first_slice():
-            h_bank(0, 0)
-            for q, copy in enumerate((nc.scalar.copy, nc.vector.tensor_copy)):
-                bank = psum_o.tile([P, HALF], F32, name="acc%d0" % q)
-                c0 = BANK + q * HALF
-                for a in range(2):
+            banks = [psum_h.tile([P, BANK], F32, name="h_bank")]
+            banks += [psum_o.tile([P, HALF], F32, name="acc%d0" % q) for q in range(2)]
+            for a in range(2):
+                h_pass(0, a, banks[0][:], 0, BANK, a == 0, a == 1)
+                for q in range(2):
                     for u in range(2):
+                        c0 = BANK + q * HALF + u * P
                         h_pass(
-                            0, a, bank[:, u * P : (u + 1) * P], c0 + u * P, c0 + (u + 1) * P,
-                            a == 0 and u == 0, a == 1 and u == 1,
+                            0, a, banks[1 + q][:, u * P : (u + 1) * P], c0, c0 + P, a == 0 and u == 0, a == 1 and u == 1
                         )
-                copy(windows[0][:, c0 : c0 + HALF], bank[:])
+            nc.scalar.copy(windows[0][:, 0:BANK], banks[0][:])
+            for q, copy in enumerate((nc.scalar.copy, nc.vector.tensor_copy)):
+                copy(windows[0][:, BANK + q * HALF : BANK + (q + 1) * HALF], banks[1 + q][:, 0:HALF])
 
         loss = {}
 
@@ -230,7 +245,7 @@ def tile_list_wildfire_layer_cession_kernel(
         first_product(1)
         turned = psum_h.tile([P, BANK], F32, name="h_bank")
         for t in range(PACK):
-            nc.tensor.transpose(turned[:, t * P : (t + 1) * P], term_rows[:, t:PASS:PACK], ident[:])
+            nc.tensor.transpose(turned[:, t * P : (t + 1) * P], term_rows[:, t, :], ident[:])
         nc.scalar.copy(terms[:], turned[:].rearrange("p (t j) -> p t j", t=PACK)[:, :, 0:6])
 
 

@@ -235,12 +235,25 @@ def tile_list_wildfire_layer_cession_kernel(
                 copies[j % 2](res[:], acc[j, half][:, 0:HALF])
                 nc.sync.dma_start(out=out[j * P : (j + 1) * P, half * HALF : (half + 1) * HALF], in_=res[:])
 
-        for quarter in range(4):
-            cs = slice(quarter * P, (quarter + 1) * P)
-            nc.gpsimd.tensor_scalar(
-                ws_il[0][:, cs, :], ws_raw[:, 0, :, cs].rearrange("p t n -> p n t"), 1.0, 0.0, ALU.mult, ALU.add
-            )
+        pieces = [divmod(k, 4) for k in range(8)]
 
+        def piece():
+            b, u = pieces.pop(0)
+            cs = slice(u * P, (u + 1) * P)
+            interleave(nc.scalar.copy, ws_il[b][:, cs, :], ws_raw[:, b, :, cs])
+
+
+        warm = psum_o.tile([P, BANK], F32, name="acc01")
+        for k in range(4):
+            nc.tensor.matmul_mx(
+                out=warm[:],
+                lhsT=w4_codes[0][:, 0, :].bitcast(U8)[:, 0 : 2 * P].bitcast(FP4X4),
+                lhsT_scale=rows[:].bitcast(U8)[:, S : S + P],
+                rhs=v_codes[0][:, BANK:S].bitcast(FP8X4),
+                rhs_scale=rows[:].bitcast(U8)[:, BANK:S],
+                start=True,
+                stop=True,
+            )
         first_slice()
         first_product(1)
         turned = psum_h.tile([P, BANK], F32, name="h_bank")
@@ -270,9 +283,9 @@ def tile_list_wildfire_layer_cession_kernel(
             if i + 2 < SLICES:
                 first_product(i + 2)
             pick_loss(i + 1)
-            if i < 4:
-                cs = slice(i * P, (i + 1) * P)
-                interleave(nc.scalar.copy, ws_il[1][:, cs, :], ws_raw[:, 1, :, cs])
+            piece()
+            if i == 4:
+                piece()
             if i > 4:
                 cs = slice((i - 5) * HALF, (i - 4) * HALF)
                 interleave(nc.scalar.copy, z_il0[:, cs, :], z_planes[0][:, :, cs])
@@ -281,15 +294,14 @@ def tile_list_wildfire_layer_cession_kernel(
             if i + 2 < SLICES:
                 pick_terms(i + 2)
             lift_whole(i + 1)
-            if i == 1:
-                quantize(ws_codes[0][:], ws_sc[0][:], ws_il[0][:])
             if i == 4:
-                quantize(ws_codes[1][:], ws_sc[1][:], ws_il[1][:])
+                quantize(ws_codes[0][:], ws_sc[0][:], ws_il[0][:])
             lay = one.tile([P, 2, PICKS], F32, name="layered")
             layered[i] = lay[:, 0, :]
             cap(layered[i], i, limit[i][:], lifted[i][:])
         money(last - 1, layered[last - 1], 0, PICKS)
         quantize(z_codes[0][:], z_sc[0][:], z_il0[:])
+        quantize(ws_codes[1][:], ws_sc[1][:], ws_il[1][:])
         for half in range(2):
             second_product(0, half)
         halves = [slice(half * HALF, (half + 1) * HALF) for half in range(2)]

@@ -82,8 +82,11 @@ def tile_list_wildfire_layer_cession_kernel(
         term_rows = held.tile([P, PACK, P], F32, name="term_rows")
         terms = held.tile([P, PACK, 6], F32, name="terms")
 
+        def place(i):
+            return i // PACK, (2, 0, 1, 3)[i % PACK]
+
         def term(v, i):
-            b, t = divmod(i, PACK)
+            b, t = place(i)
             return terms[:, t, 2 * v + b : 2 * v + b + 1]
 
         windows = []
@@ -139,7 +142,7 @@ def tile_list_wildfire_layer_cession_kernel(
         ws_il = [held.tile([P, N, PACK], BF16, name="ws_il%d" % b, align_bytes=64) for b in range(2)]
         ws_codes = [held.tile([P, N], U32, name="ws_codes%d" % b, align_bytes=64) for b in range(2)]
         ws_sc = [held.tile([P, N], U8, name="ws_sc%d" % b, align_bytes=64) for b in range(2)]
-        z_planes = [held.tile([P, PACK, PICKS], BF16, name="z_planes%d" % b, align_bytes=64) for b in range(2)]
+        z_pairs = [held.tile([P, 2, PICKS, 2], BF16, name="z_pairs%d" % b, align_bytes=64) for b in range(2)]
         HALF = PICKS // 2
         z_il0 = held.tile([P, PICKS, PACK], BF16, name="z_il0", align_bytes=64)
         z_codes = [held.tile([P, PICKS], U32, name="z_codes%d" % b, align_bytes=64) for b in range(2)]
@@ -148,11 +151,17 @@ def tile_list_wildfire_layer_cession_kernel(
         def interleave(copy, dst, src):
             copy(dst.rearrange("p (c i) t -> p c t i", i=4), src.rearrange("p t (c i) -> p c t i", i=4))
 
+        def weave(copy, dst, b, cs):
+            copy(
+                dst.rearrange("p c t -> p (c t)").bitcast(U32).rearrange("p (c u) -> p c u", u=2),
+                z_pairs[b][:].rearrange("p u c e -> p u (c e)").bitcast(U32)[:, :, cs].rearrange("p u c -> p c u"),
+            )
+
         def quantize(codes, scales, il):
             nc.vector.quantize_mx(out=codes.bitcast(FP8X4), scales=scales, in_=il.rearrange("p n t -> p (n t)"))
 
         def h_pass(i, a, dst, c0, c1, start, stop):
-            b, t = divmod(i, PACK)
+            b, t = place(i)
             if b == 0:
                 w4_plane = planes_early[:, a, :].bitcast(U8)[:, S + P * t : S + P * (t + 1)]
             else:
@@ -208,10 +217,11 @@ def tile_list_wildfire_layer_cession_kernel(
             nc.vector.scalar_tensor_tensor(dst, limit, term(1, i), lifted, ALU.add, ALU.min)
 
         def money(i, layered, c0, c1):
-            b, t = divmod(i, PACK)
-            nc.scalar.activation(z_planes[b][:, t, c0:c1], layered, ACT.Copy, scale=term(2, i))
+            b, t = place(i)
+            nc.scalar.activation(z_pairs[b][:, t // 2, c0:c1, t % 2], layered, ACT.Copy, scale=term(2, i))
 
         acc = {}
+        ws_block = {(b, j): ws_codes[b][:, j * P : (j + 1) * P] for b in range(2) for j in range(4)}
 
         def second_product(b, half):
             for j in range(N // P):
@@ -221,7 +231,7 @@ def tile_list_wildfire_layer_cession_kernel(
                     acc[j, half] = psum_h.tile([P, BANK], F32, name="h_bank")
                 nc.tensor.matmul_mx(
                     out=acc[j, half][:, 0:HALF],
-                    lhsT=ws_codes[b][:, j * P : (j + 1) * P].bitcast(FP8X4),
+                    lhsT=ws_block[b, j].bitcast(FP8X4),
                     lhsT_scale=ws_sc[b][:, j * P : (j + 1) * P],
                     rhs=z_codes[b][:, half * HALF : (half + 1) * HALF].bitcast(FP8X4),
                     rhs_scale=z_sc[b][:, half * HALF : (half + 1) * HALF],
@@ -229,13 +239,18 @@ def tile_list_wildfire_layer_cession_kernel(
                     stop=(b == 1),
                 )
 
-        def store(half, copies):
-            for j in range(N // P):
-                res = held.tile([P, HALF], F32, name="res%d%d" % (j, half))
-                copies[j % 2](res[:], acc[j, half][:, 0:HALF])
-                nc.sync.dma_start(out=out[j * P : (j + 1) * P, half * HALF : (half + 1) * HALF], in_=res[:])
+        out_view = out.rearrange("(j p) m -> p j m", p=P)
 
-        pieces = [divmod(k, 4) for k in range(8)]
+        def store(half):
+            for pair in range(2):
+                res = held.tile([P, 2, HALF], F32, name="res%d%d" % (pair, half))
+                for u, copy in enumerate((nc.scalar.copy, nc.vector.tensor_copy)):
+                    copy(res[:, u, :], acc[2 * pair + u, half][:, 0:HALF])
+                nc.sync.dma_start(
+                    out=out_view[:, 2 * pair : 2 * pair + 2, half * HALF : (half + 1) * HALF], in_=res[:]
+                )
+
+        pieces = [divmod(k, 4) for k in range(7)]
 
         def piece():
             b, u = pieces.pop(0)
@@ -266,7 +281,10 @@ def tile_list_wildfire_layer_cession_kernel(
 
         def pick_terms(i):
             attach[i] = ring.tile([P, PICKS], F32, name="attach")
-            limit[i] = ring.tile([P, PICKS], F32, name="limit", bufs=4)
+            if i == SLICES - 1:
+                limit[i] = held.tile([P, PICKS], F32, name="limit7", align_bytes=64)
+            else:
+                limit[i] = ring.tile([P, PICKS], F32, name="limit", bufs=4)
             pick(attach[i][:], i, pos2_t, 0, PICKS)
             pick(limit[i][:], i, pos3_t, 0, PICKS)
 
@@ -284,11 +302,9 @@ def tile_list_wildfire_layer_cession_kernel(
                 first_product(i + 2)
             pick_loss(i + 1)
             piece()
-            if i == 4:
-                piece()
             if i > 4:
                 cs = slice((i - 5) * HALF, (i - 4) * HALF)
-                interleave(nc.scalar.copy, z_il0[:, cs, :], z_planes[0][:, :, cs])
+                weave(nc.scalar.copy, z_il0[:, cs, :], 0, cs)
             if i >= 1:
                 money(i - 1, layered[i - 1], 0, PICKS)
             if i + 2 < SLICES:
@@ -296,26 +312,32 @@ def tile_list_wildfire_layer_cession_kernel(
             lift_whole(i + 1)
             if i == 4:
                 quantize(ws_codes[0][:], ws_sc[0][:], ws_il[0][:])
-            lay = one.tile([P, 2, PICKS], F32, name="layered")
-            layered[i] = lay[:, 0, :]
+            lay = one.tile([P, PICKS], F32, name="layered", align_bytes=64)
+            layered[i] = lay[:, :]
             cap(layered[i], i, limit[i][:], lifted[i][:])
         money(last - 1, layered[last - 1], 0, PICKS)
         quantize(z_codes[0][:], z_sc[0][:], z_il0[:])
-        quantize(ws_codes[1][:], ws_sc[1][:], ws_il[1][:])
+        quantize(ws_codes[1][:, 2 * P : 3 * P], ws_sc[1][:, 2 * P : 3 * P], ws_il[1][:, 2 * P : 3 * P, :])
+        ws_il_last = one.tile([P, P, PACK], BF16, name="ws_il_last", tag="layered", align_bytes=64)
+        interleave(nc.scalar.copy, ws_il_last[:], ws_raw[:, 1, :, 3 * P : 4 * P])
+        lay = held.tile([P, PICKS], F32, name="lay7")
         for half in range(2):
             second_product(0, half)
         halves = [slice(half * HALF, (half + 1) * HALF) for half in range(2)]
         for cs in halves:
-            cap(lay[:, 1, cs], last, limit[last][:, cs], lifted[last][:, cs])
+            cap(lay[:, cs], last, limit[last][:, cs], lifted[last][:, cs])
         for cs in halves:
-            nc.vector.tensor_scalar(z_planes[1][:, PACK - 1, cs], lay[:, 1, cs], term(2, last), None, ALU.mult)
-        z_il1 = held.tile([P, PICKS, PACK], BF16, name="z_il1", align_bytes=64)
-        SHARE = HALF + 96
-        interleave(nc.vector.tensor_copy, z_il1[:, 0:HALF, :], z_planes[1][:, :, 0:HALF])
-        interleave(nc.vector.tensor_copy, z_il1[:, HALF:SHARE, :], z_planes[1][:, :, HALF:SHARE])
-        interleave(nc.scalar.copy, z_il1[:, SHARE:PICKS, :], z_planes[1][:, :, SHARE:PICKS])
-        for cs in halves:
-            quantize(z_codes[1][:, cs], z_sc[1][:, cs], z_il1[:, cs, :])
+            nc.vector.tensor_scalar(z_pairs[1][:, 1, cs, 1], lay[:, cs], term(2, last), None, ALU.mult)
+        z_il1 = [held.tile([P, HALF, PACK], BF16, name="z_il1%d" % half, align_bytes=64) for half in range(2)]
+        ws_front = held.tile([P, HALF], U32, name="ws_front", tag="limit7", align_bytes=64)
+        quantize(ws_front[:], ws_sc[1][:, 0:HALF], ws_il[1][:, 0:HALF, :])
+        for j in range(2):
+            ws_block[1, j] = ws_front[:, j * P : (j + 1) * P]
+        for half, copy in enumerate((nc.vector.tensor_copy, nc.scalar.copy)):
+            weave(copy, z_il1[half][:], 1, halves[half])
+        quantize(ws_codes[1][:, 3 * P : 4 * P], ws_sc[1][:, 3 * P : 4 * P], ws_il_last[:])
+        for half, cs in enumerate(halves):
+            quantize(z_codes[1][:, cs], z_sc[1][:, cs], z_il1[half][:])
         for half in range(2):
             second_product(1, half)
-            store(half, (nc.scalar.copy, nc.vector.tensor_copy))
+            store(half)

@@ -244,13 +244,13 @@ def tile_list_wildfire_layer_cession_kernel(
         def store(half):
             for pair in range(2):
                 res = held.tile([P, 2, HALF], F32, name="res%d%d" % (pair, half))
-                for u, copy in enumerate((nc.scalar.copy, nc.vector.tensor_copy)):
+                for u, copy in enumerate((nc.scalar.copy, (nc.scalar.copy, nc.vector.tensor_copy)[half])):
                     copy(res[:, u, :], acc[2 * pair + u, half][:, 0:HALF])
                 nc.sync.dma_start(
                     out=out_view[:, 2 * pair : 2 * pair + 2, half * HALF : (half + 1) * HALF], in_=res[:]
                 )
 
-        pieces = [divmod(k, 4) for k in range(7)]
+        pieces = [divmod(k, 4) for k in range(8)]
 
         def piece():
             b, u = pieces.pop(0)
@@ -278,66 +278,71 @@ def tile_list_wildfire_layer_cession_kernel(
 
 
         attach, limit, lifted, layered = {}, {}, {}, {}
+        last = SLICES - 1
+        halves = [slice(half * HALF, (half + 1) * HALF) for half in range(2)]
 
         def pick_terms(i):
             attach[i] = ring.tile([P, PICKS], F32, name="attach")
-            if i == SLICES - 1:
-                limit[i] = held.tile([P, PICKS], F32, name="limit7", align_bytes=64)
-            else:
-                limit[i] = ring.tile([P, PICKS], F32, name="limit", bufs=4)
-            pick(attach[i][:], i, pos2_t, 0, PICKS)
-            pick(limit[i][:], i, pos3_t, 0, PICKS)
+            limit[i] = ring.tile([P, PICKS], F32, name="limit", bufs=4)
+            end = HALF if i == last else PICKS
+            pick(attach[i][:, 0:end], i, pos2_t, 0, end)
+            pick(limit[i][:, 0:end], i, pos3_t, 0, end)
 
         def lift_whole(i):
             lifted[i] = ring.tile([P, PICKS], F32, name="lifted")
-            lift(lifted[i][:], i, attach[i][:], 0, PICKS)
+            end = HALF if i == last else PICKS
+            lift(lifted[i][:, 0:end], i, attach[i][:, 0:end], 0, end)
 
+        first, second = halves
         pick_terms(0)
         pick_loss(0)
         pick_terms(1)
         lift_whole(0)
-        last = SLICES - 1
-        for i in range(last):
-            if i + 2 < SLICES:
-                first_product(i + 2)
+        for i in range(last - 1):
+            first_product(i + 2)
             pick_loss(i + 1)
-            piece()
-            if i > 4:
-                cs = slice((i - 5) * HALF, (i - 4) * HALF)
-                weave(nc.scalar.copy, z_il0[:, cs, :], 0, cs)
+            for k in range((2, 1, 1, 2, 1, 1)[i]):
+                piece()
             if i >= 1:
                 money(i - 1, layered[i - 1], 0, PICKS)
-            if i + 2 < SLICES:
-                pick_terms(i + 2)
+            pick_terms(i + 2)
             lift_whole(i + 1)
-            if i == 4:
+            if i == 2:
                 quantize(ws_codes[0][:], ws_sc[0][:], ws_il[0][:])
+            if i >= 4:
+                cs = halves[i - 4]
+                quantize(ws_codes[1][:, cs], ws_sc[1][:, cs], ws_il[1][:, cs, :])
             lay = one.tile([P, PICKS], F32, name="layered", align_bytes=64)
             layered[i] = lay[:, :]
             cap(layered[i], i, limit[i][:], lifted[i][:])
-        money(last - 1, layered[last - 1], 0, PICKS)
-        quantize(z_codes[0][:], z_sc[0][:], z_il0[:])
-        quantize(ws_codes[1][:, 2 * P : 3 * P], ws_sc[1][:, 2 * P : 3 * P], ws_il[1][:, 2 * P : 3 * P, :])
-        ws_il_last = one.tile([P, P, PACK], BF16, name="ws_il_last", tag="layered", align_bytes=64)
-        interleave(nc.scalar.copy, ws_il_last[:], ws_raw[:, 1, :, 3 * P : 4 * P])
-        lay = held.tile([P, PICKS], F32, name="lay7")
-        for half in range(2):
-            second_product(0, half)
-        halves = [slice(half * HALF, (half + 1) * HALF) for half in range(2)]
-        for cs in halves:
-            cap(lay[:, cs], last, limit[last][:, cs], lifted[last][:, cs])
-        for cs in halves:
-            nc.vector.tensor_scalar(z_pairs[1][:, 1, cs, 1], lay[:, cs], term(2, last), None, ALU.mult)
+        pick_loss(last)
+        weave(nc.scalar.copy, z_il0[:, first, :], 0, first)
+        money(last - 2, layered[last - 2], 0, PICKS)
+        lift_whole(last)
+        lay6 = windows[last % WINDOWS][:, S : S + PICKS]
+        cap(lay6, last - 1, limit[last - 1][:], lifted[last - 1][:])
+        quantize(z_codes[0][:, first], z_sc[0][:, first], z_il0[:, first, :])
+        second_product(0, 0)
+        lay7 = held.tile([P, PICKS], F32, name="lay7")
+        cap(lay7[:, first], last, limit[last][:, first], lifted[last][:, first])
+        money(last - 1, lay6[:, first], 0, HALF)
+        money(last, lay7[:, first], 0, HALF)
         z_il1 = [held.tile([P, HALF, PACK], BF16, name="z_il1%d" % half, align_bytes=64) for half in range(2)]
-        ws_front = held.tile([P, HALF], U32, name="ws_front", tag="limit7", align_bytes=64)
-        quantize(ws_front[:], ws_sc[1][:, 0:HALF], ws_il[1][:, 0:HALF, :])
-        for j in range(2):
-            ws_block[1, j] = ws_front[:, j * P : (j + 1) * P]
-        for half, copy in enumerate((nc.vector.tensor_copy, nc.scalar.copy)):
-            weave(copy, z_il1[half][:], 1, halves[half])
-        quantize(ws_codes[1][:, 3 * P : 4 * P], ws_sc[1][:, 3 * P : 4 * P], ws_il_last[:])
-        for half, cs in enumerate(halves):
-            quantize(z_codes[1][:, cs], z_sc[1][:, cs], z_il1[half][:])
-        for half in range(2):
-            second_product(1, half)
-            store(half)
+        weave(nc.scalar.copy, z_il1[0][:], 1, first)
+        late_attach, late_limit = limit[last - 1][:, first], limit[last - 1][:, second]
+        pick(late_attach, last, pos2_t, HALF, PICKS)
+        pick(late_limit, last, pos3_t, HALF, PICKS)
+        money(last - 1, lay6[:, second], HALF, PICKS)
+        weave(nc.scalar.copy, z_il0[:, second, :], 0, second)
+        lift(lay7[:, first], last, late_attach, HALF, PICKS)
+        quantize(z_codes[1][:, first], z_sc[1][:, first], z_il1[0][:])
+        second_product(1, 0)
+        cap(lay7[:, second], last, late_limit, lay7[:, first])
+        quantize(z_codes[0][:, second], z_sc[0][:, second], z_il0[:, second, :])
+        second_product(0, 1)
+        nc.vector.tensor_scalar(z_pairs[1][:, 1, second, 1], lay7[:, second], term(2, last), None, ALU.mult)
+        store(0)
+        weave(nc.vector.tensor_copy, z_il1[1][:], 1, second)
+        quantize(z_codes[1][:, second], z_sc[1][:, second], z_il1[1][:])
+        second_product(1, 1)
+        store(1)

@@ -44,21 +44,24 @@ def tile_list_wildfire_layer_cession_kernel(
 
         w4_sc_raw = held.tile([P, H // 4], I32, name="w4_sc_raw", align_bytes=64)
         tab_sc = held.tile([P, T // 4], I32, name="tab_sc", align_bytes=64)
-        for raw, scales in ((tab_sc, tab_scales), (w4_sc_raw, w4_scales)):
-            for a in range(2):
-                nc.sync.dma_start(
-                    out=raw[a:32:2, :], in_=scales[a].rearrange("(u r) n -> r u n", r=4).bitcast(I32)
-                )
         w4_view = w4_words.rearrange("a p n -> p a n").bitcast(I32)
         w4_raw0 = held.tile([P, 2, H // 4], I32, name="w4_raw0", align_bytes=64)
-        nc.sync.dma_start(offs_t[:], offs)
+        tab_w = [one.tile([P, T], I32, name="tab_w%d" % a, tag="big%d" % a, align_bytes=64) for a in range(2)]
+
+        def load_scales(raw, scales):
+            for a in range(2):
+                nc.sync.dma_start(out=raw[a:32:2, :], in_=scales[a].bitcast(I32))
+
+        def load_table(a):
+            nc.sync.dma_start(out=tab_w[a][:], in_=tab_words[a].rearrange("p t i -> p (t i)").bitcast(I32))
+
         nc.sync.dma_start(out=w4_raw0[:], in_=w4_view[:, :, 0 : H // 4])
-        tab_w = []
-        for a in range(2):
-            tile_a = one.tile([P, T], I32, name="tab_w%d" % a, tag="big%d" % a, align_bytes=64)
-            nc.sync.dma_start(out=tile_a[:], in_=tab_words[a].rearrange("p t i -> p (t i)").bitcast(I32))
-            tab_w.append(tile_a)
+        load_scales(tab_sc, tab_scales)
+        nc.sync.dma_start(offs_t[:], offs)
+        load_table(0)
+        load_scales(w4_sc_raw, w4_scales)
         nc.sync.dma_start(pos1_t[:], pos1)
+        load_table(1)
         nc.sync.dma_start(pos2_t[:], pos2)
         nc.sync.dma_start(pos3_t[:], pos3)
 
@@ -69,9 +72,7 @@ def tile_list_wildfire_layer_cession_kernel(
             nc.vector.memset(raw[64:128, :], 0)
         EARLY = S + PASS
         planes_early = held.tile([P, 2, EARLY // 4], I32, name="planes_early", align_bytes=64)
-        planes_late = held.tile([P, 2, PASS // 4], I32, name="planes_late", align_bytes=64)
         nc.gpsimd.memset(planes_early[:], 0)
-        nc.gpsimd.memset(planes_late[:], 0)
 
         term_raw = held.tile([P, PASS], F32, name="term_raw")
         nc.gpsimd.memset(term_raw[:], 0.0)
@@ -115,12 +116,10 @@ def tile_list_wildfire_layer_cession_kernel(
             )
 
         nc.vector.tensor_copy(rows[:, 0 : S // 4], v_sc_rows[:].bitcast(I32))
-        for q in range(4):
-            nc.sync.dma_start(out=planes_early[q:P:32, :, :], in_=rows[8 * q : 8 * q + 8, 0 : EARLY // 4])
+        for q in (0, 2, 1, 3):
+            nc.sync.dma_start(out=planes_early[32 * q : 32 * q + 4, :, :], in_=rows[8 * q : 8 * q + 8, 0 : EARLY // 4])
         w4_raw1 = one.tile([P, 2, H // 4], I32, name="w4_raw1", tag="late", align_bytes=64)
         nc.sync.dma_start(out=w4_raw1[:], in_=w4_view[:, :, H // 4 : H // 2])
-        for q in range(4):
-            nc.sync.dma_start(out=planes_late[q:P:32, :, :], in_=rows[8 * q : 8 * q + 8, EARLY // 4 :])
         order_columns(0, w4_raw0)
 
         v_codes = []
@@ -136,9 +135,14 @@ def tile_list_wildfire_layer_cession_kernel(
 
         ws_raw = one.tile([P, 2, PACK, N], F32, name="ws_raw", tag="big0", align_bytes=64)
         ws_view = ws.rearrange("(b g t q) n -> b t g q n", b=2, t=PACK, q=8)
-        for b in range(2):
-            for t in range(PACK):
-                nc.sync.dma_start(out=ws_raw[:, b, t, :], in_=ws_view[b, t])
+        for t in range(PACK):
+            nc.sync.dma_start(out=ws_raw[:, 0, t, :], in_=ws_view[0, t])
+        planes_late = one.tile([P, 2, PASS // 4], I32, name="planes_late", tag="big1", align_bytes=64)
+        nc.gpsimd.memset(planes_late[:], 0)
+        for t in range(PACK):
+            nc.sync.dma_start(out=ws_raw[:, 1, t, :], in_=ws_view[1, t])
+        for q in (0, 2, 1, 3):
+            nc.sync.dma_start(out=planes_late[32 * q : 32 * q + 4, :, :], in_=rows[8 * q : 8 * q + 8, EARLY // 4 :])
         ws_il = [held.tile([P, N, PACK], BF16, name="ws_il%d" % b, align_bytes=64) for b in range(2)]
         ws_codes = [held.tile([P, N], U32, name="ws_codes%d" % b, align_bytes=64) for b in range(2)]
         ws_sc = [held.tile([P, N], U8, name="ws_sc%d" % b, align_bytes=64) for b in range(2)]
@@ -198,7 +202,7 @@ def tile_list_wildfire_layer_cession_kernel(
                             0, a, banks[1 + q][:, u * P : (u + 1) * P], c0, c0 + P, a == 0 and u == 0, a == 1 and u == 1
                         )
             nc.scalar.copy(windows[0][:, 0:BANK], banks[0][:])
-            for q, copy in enumerate((nc.scalar.copy, nc.vector.tensor_copy)):
+            for q, copy in enumerate((nc.vector.tensor_copy, nc.scalar.copy)):
                 copy(windows[0][:, BANK + q * HALF : BANK + (q + 1) * HALF], banks[1 + q][:, 0:HALF])
 
         loss = {}
@@ -250,7 +254,10 @@ def tile_list_wildfire_layer_cession_kernel(
                     out=out_view[:, 2 * pair : 2 * pair + 2, half * HALF : (half + 1) * HALF], in_=res[:]
                 )
 
-        pieces = [divmod(k, 4) for k in range(8)]
+        pieces = [(1, u) for u in range(4)]
+        nc.gpsimd.tensor_scalar(
+            ws_il[0][:], ws_raw[:, 0, :, :].rearrange("p t n -> p n t"), 1.0, 0.0, ALU.mult, ALU.add
+        )
 
         def piece():
             b, u = pieces.pop(0)
@@ -301,7 +308,7 @@ def tile_list_wildfire_layer_cession_kernel(
         for i in range(last - 1):
             first_product(i + 2)
             pick_loss(i + 1)
-            for k in range((2, 1, 1, 2, 1, 1)[i]):
+            for k in range((0, 1, 1, 1, 1, 0)[i]):
                 piece()
             if i >= 1:
                 money(i - 1, layered[i - 1], 0, PICKS)

@@ -143,22 +143,20 @@ def tile_list_wildfire_layer_cession_kernel(
             nc.sync.dma_start(out=ws_raw[:, 1, t, :], in_=ws_view[1, t])
         for q in (0, 2, 1, 3):
             nc.sync.dma_start(out=planes_late[32 * q : 32 * q + 4, :, :], in_=rows[8 * q : 8 * q + 8, EARLY // 4 :])
-        ws_il = [held.tile([P, N, PACK], BF16, name="ws_il%d" % b, align_bytes=64) for b in range(2)]
-        ws_codes = [held.tile([P, N], U32, name="ws_codes%d" % b, align_bytes=64) for b in range(2)]
         ws_sc = [held.tile([P, N], U8, name="ws_sc%d" % b, align_bytes=64) for b in range(2)]
-        z_pairs = [held.tile([P, 2, PICKS, 2], BF16, name="z_pairs%d" % b, align_bytes=64) for b in range(2)]
         HALF = PICKS // 2
-        z_il0 = held.tile([P, PICKS, PACK], BF16, name="z_il0", align_bytes=64)
+        z_pairs = [held.tile([P, 2, 2, HALF, 2], BF16, name="z_pairs%d" % b, align_bytes=64) for b in range(2)]
+        z_il0 = held.tile([P, HALF, PACK], BF16, name="z_il0", align_bytes=64)
         z_codes = [held.tile([P, PICKS], U32, name="z_codes%d" % b, align_bytes=64) for b in range(2)]
         z_sc = [held.tile([P, PICKS], U8, name="z_sc%d" % b, align_bytes=64) for b in range(2)]
 
         def interleave(copy, dst, src):
             copy(dst.rearrange("p (c i) t -> p c t i", i=4), src.rearrange("p t (c i) -> p c t i", i=4))
 
-        def weave(copy, dst, b, cs):
+        def weave(copy, dst, b, half):
             copy(
                 dst.rearrange("p c t -> p (c t)").bitcast(U32).rearrange("p (c u) -> p c u", u=2),
-                z_pairs[b][:].rearrange("p u c e -> p u (c e)").bitcast(U32)[:, :, cs].rearrange("p u c -> p c u"),
+                z_pairs[b][:, half].rearrange("p u c e -> p u (c e)").bitcast(U32).rearrange("p u c -> p c u"),
             )
 
         def quantize(codes, scales, il):
@@ -208,7 +206,7 @@ def tile_list_wildfire_layer_cession_kernel(
         loss = {}
 
         def pick_loss(i):
-            loss[i] = ring.tile([P, PICKS], F32, name="loss")
+            loss[i] = ring.tile([P, PICKS], F32, name="loss", bufs=4)
             nc.scalar.activation(loss[i][:], windows[i % WINDOWS][:].indirect(pos1_t[:]), ACT.Exp)
 
         def pick(dst, i, pos_t, c0, c1):
@@ -222,10 +220,15 @@ def tile_list_wildfire_layer_cession_kernel(
 
         def money(i, layered, c0, c1):
             b, t = place(i)
-            nc.scalar.activation(z_pairs[b][:, t // 2, c0:c1, t % 2], layered, ACT.Copy, scale=term(2, i))
+            dst = z_pairs[b][:, c0 // HALF : c1 // HALF, t // 2, :, t % 2]
+            src = layered.rearrange("p (h c) -> p h c", c=HALF)
+            if i == 4:
+                nc.gpsimd.tensor_scalar(dst, src, term(2, i), 0.0, ALU.mult, ALU.add)
+            else:
+                nc.scalar.activation(dst, src, ACT.Copy, scale=term(2, i))
 
         acc = {}
-        ws_block = {(b, j): ws_codes[b][:, j * P : (j + 1) * P] for b in range(2) for j in range(4)}
+        ws_block = {}
 
         def second_product(b, half):
             for j in range(N // P):
@@ -254,16 +257,21 @@ def tile_list_wildfire_layer_cession_kernel(
                     out=out_view[:, 2 * pair : 2 * pair + 2, half * HALF : (half + 1) * HALF], in_=res[:]
                 )
 
-        pieces = [(1, u) for u in range(4)]
-        nc.gpsimd.tensor_scalar(
-            ws_il[0][:], ws_raw[:, 0, :, :].rearrange("p t n -> p n t"), 1.0, 0.0, ALU.mult, ALU.add
-        )
+        ws_il = {}
+        ws_parts = ((0, 0, N), (1, 0, N // 2), (1, N // 2, N))
 
-        def piece():
-            b, u = pieces.pop(0)
-            cs = slice(u * P, (u + 1) * P)
-            interleave(nc.scalar.copy, ws_il[b][:, cs, :], ws_raw[:, b, :, cs])
+        def round_ws(k, tag):
+            b, c0, c1 = ws_parts[k]
+            ws_il[k] = one.tile([P, c1 - c0, PACK], BF16, name="ws_il%d" % k, tag=tag, align_bytes=64)
+            src = ws_raw[:, b, :, c0:c1]
+            nc.gpsimd.tensor_scalar(ws_il[k][:], src.rearrange("p t n -> p n t"), 1.0, 0.0, ALU.mult, ALU.add)
 
+        def quantize_ws(k, tag):
+            b, c0, c1 = ws_parts[k]
+            codes = one.tile([P, c1 - c0], U32, name="ws_codes%d" % k, tag=tag, align_bytes=64)
+            quantize(codes[:], ws_sc[b][:, c0:c1], ws_il[k][:])
+            for u in range((c1 - c0) // P):
+                ws_block[b, c0 // P + u] = codes[:, u * P : (u + 1) * P]
 
         warm = psum_o.tile([P, BANK], F32, name="acc01")
         for k in range(4):
@@ -288,68 +296,102 @@ def tile_list_wildfire_layer_cession_kernel(
         last = SLICES - 1
         halves = [slice(half * HALF, (half + 1) * HALF) for half in range(2)]
 
-        def pick_terms(i):
-            attach[i] = ring.tile([P, PICKS], F32, name="attach")
-            limit[i] = ring.tile([P, PICKS], F32, name="limit", bufs=4)
+        def pick_attach(i):
+            attach[i] = one.tile([P, PICKS], F32, name="attach%d" % i, tag="attach%d" % i, align_bytes=64)
             end = HALF if i == last else PICKS
             pick(attach[i][:, 0:end], i, pos2_t, 0, end)
+
+        def pick_limit(i):
+            limit[i] = one.tile([P, PICKS], F32, name="limit%d" % i, tag="limit%d" % i, align_bytes=64)
+            end = HALF if i == last else PICKS
             pick(limit[i][:, 0:end], i, pos3_t, 0, end)
 
+        lift_bufs = [held.tile([P, PICKS], F32, name="lift_buf%d" % k) for k in range(3)]
+        lay_bufs = [held.tile([P, PICKS], F32, name="lay_buf%d" % k) for k in range(2)]
+
         def lift_whole(i):
-            lifted[i] = ring.tile([P, PICKS], F32, name="lifted")
+            lifted[i] = lift_bufs[2 if i == last else i // 2 % 2]
             end = HALF if i == last else PICKS
             lift(lifted[i][:, 0:end], i, attach[i][:, 0:end], 0, end)
 
-        first, second = halves
-        pick_terms(0)
-        pick_loss(0)
-        pick_terms(1)
-        lift_whole(0)
-        for i in range(last - 1):
-            first_product(i + 2)
-            pick_loss(i + 1)
-            for k in range((0, 1, 1, 1, 1, 0)[i]):
-                piece()
-            if i >= 1:
-                money(i - 1, layered[i - 1], 0, PICKS)
-            pick_terms(i + 2)
-            lift_whole(i + 1)
-            if i == 2:
-                quantize(ws_codes[0][:], ws_sc[0][:], ws_il[0][:])
-            if i >= 4:
-                cs = halves[i - 4]
-                quantize(ws_codes[1][:, cs], ws_sc[1][:, cs], ws_il[1][:, cs, :])
-            lay = one.tile([P, PICKS], F32, name="layered", align_bytes=64)
-            layered[i] = lay[:, :]
+        excess = {}
+
+        def pick_excess(i):
+            excess[i] = ring.tile([P, PICKS], F32, name="excess", bufs=2)
+            nc.vector.tensor_tensor(excess[i][:], windows[i % WINDOWS][:].indirect(pos2_t[:]), loss[i][:], ALU.subtract)
+
+        def lift_by_excess(i):
+            rise = ring.tile([P, PICKS], F32, name="rise", bufs=2)
+            nc.scalar.activation(rise[:], excess[i][:], ACT.Relu, bias=term(0, i))
+            lifted[i] = lift_bufs[i // 2 % 2]
+            nc.gpsimd.tensor_tensor(lifted[i][:], loss[i][:], rise[:], ALU.add)
+
+        def cap_whole(i):
+            layered[i] = lay_bufs[i % 2][:, :]
             cap(layered[i], i, limit[i][:], lifted[i][:])
+
+        first, second = halves
+        round_ws(0, "ws_il0")
+        for k in range(3):
+            a, b = 2 * k, 2 * k + 1
+            pick_attach(a)
+            pick_limit(a)
+            pick_limit(b)
+            pick_loss(a)
+            pick_loss(b)
+            lift_whole(a)
+            pick_excess(b)
+            quantize_ws(k, "attach%d" % a)
+            if k >= 2:
+                money(b - 4, layered[b - 4], 0, PICKS)
+            if k >= 1:
+                cap_whole(b - 2)
+                money(a - 2, layered[a - 2], 0, PICKS)
+            cap_whole(a)
+            if k < 2:
+                round_ws(k + 1, "limit%d" % a)
+            else:
+                money(a, layered[a], 0, PICKS)
+            first_product(a + 2)
+            lift_by_excess(b)
+            first_product(b + 2)
+        pick_attach(last - 1)
+        pick_limit(last - 1)
+        pick_attach(last)
+        pick_limit(last)
+        pick_loss(last - 1)
+        lift_whole(last - 1)
+        money(last - 4, layered[last - 4], 0, PICKS)
+        cap_whole(last - 2)
         pick_loss(last)
-        weave(nc.scalar.copy, z_il0[:, first, :], 0, first)
+        weave(nc.scalar.copy, z_il0[:], 0, 0)
         money(last - 2, layered[last - 2], 0, PICKS)
         lift_whole(last)
         lay6 = windows[last % WINDOWS][:, S : S + PICKS]
         cap(lay6, last - 1, limit[last - 1][:], lifted[last - 1][:])
-        quantize(z_codes[0][:, first], z_sc[0][:, first], z_il0[:, first, :])
+        quantize(z_codes[0][:, first], z_sc[0][:, first], z_il0[:])
         second_product(0, 0)
-        lay7 = held.tile([P, PICKS], F32, name="lay7")
+        lay7 = lay_bufs[0]
         cap(lay7[:, first], last, limit[last][:, first], lifted[last][:, first])
         money(last - 1, lay6[:, first], 0, HALF)
         money(last, lay7[:, first], 0, HALF)
         z_il1 = [held.tile([P, HALF, PACK], BF16, name="z_il1%d" % half, align_bytes=64) for half in range(2)]
-        weave(nc.scalar.copy, z_il1[0][:], 1, first)
+        weave(nc.scalar.copy, z_il1[0][:], 1, 0)
         late_attach, late_limit = limit[last - 1][:, first], limit[last - 1][:, second]
         pick(late_attach, last, pos2_t, HALF, PICKS)
         pick(late_limit, last, pos3_t, HALF, PICKS)
         money(last - 1, lay6[:, second], HALF, PICKS)
-        weave(nc.scalar.copy, z_il0[:, second, :], 0, second)
+        z_il0_late = z_pairs[1][:, 0].rearrange("p u c e -> p (u c e)").rearrange("p (c t) -> p c t", t=PACK)
+        weave(nc.scalar.copy, z_il0_late, 0, 1)
         lift(lay7[:, first], last, late_attach, HALF, PICKS)
         quantize(z_codes[1][:, first], z_sc[1][:, first], z_il1[0][:])
         second_product(1, 0)
         cap(lay7[:, second], last, late_limit, lay7[:, first])
-        quantize(z_codes[0][:, second], z_sc[0][:, second], z_il0[:, second, :])
+        quantize(z_codes[0][:, second], z_sc[0][:, second], z_il0_late)
         second_product(0, 1)
-        nc.vector.tensor_scalar(z_pairs[1][:, 1, second, 1], lay7[:, second], term(2, last), None, ALU.mult)
+        nc.vector.tensor_scalar(z_pairs[1][:, 1, 1, :, 1], lay7[:, second], term(2, last), None, ALU.mult)
         store(0)
-        weave(nc.vector.tensor_copy, z_il1[1][:], 1, second)
+        weave(nc.vector.tensor_copy, z_il1[1][:], 1, 1)
         quantize(z_codes[1][:, second], z_sc[1][:, second], z_il1[1][:])
         second_product(1, 1)
         store(1)

@@ -34,7 +34,7 @@ def tile_list_wildfire_layer_cession_kernel(
         held = ctx.enter_context(tc.tile_pool(name="held", bufs=1))
         ring = ctx.enter_context(tc.tile_pool(name="ring", bufs=3))
         one = ctx.enter_context(tc.tile_pool(name="one", bufs=1))
-        psum_h = ctx.enter_context(tc.psum_pool(name="psum_h", bufs=2))
+        psum_h = ctx.enter_context(tc.psum_pool(name="psum_h", bufs=4))
         psum_o = ctx.enter_context(tc.psum_pool(name="psum_o", bufs=1))
 
         offs_t = held.tile([P, S // 16], U16, name="offs_t")
@@ -84,7 +84,7 @@ def tile_list_wildfire_layer_cession_kernel(
         terms = held.tile([P, PACK, 6], F32, name="terms")
 
         def place(i):
-            return i // PACK, (2, 0, 1, 3)[i % PACK]
+            return ((0, 2), (0, 0), (0, 1), (1, 2), (0, 3), (1, 0), (1, 1), (1, 3))[i]
 
         def term(v, i):
             b, t = place(i)
@@ -139,24 +139,24 @@ def tile_list_wildfire_layer_cession_kernel(
             nc.sync.dma_start(out=ws_raw[:, 0, t, :], in_=ws_view[0, t])
         planes_late = one.tile([P, 2, PASS // 4], I32, name="planes_late", tag="big1", align_bytes=64)
         nc.gpsimd.memset(planes_late[:], 0)
-        for t in range(PACK):
-            nc.sync.dma_start(out=ws_raw[:, 1, t, :], in_=ws_view[1, t])
         for q in (0, 2, 1, 3):
             nc.sync.dma_start(out=planes_late[32 * q : 32 * q + 4, :, :], in_=rows[8 * q : 8 * q + 8, EARLY // 4 :])
+        for t in range(PACK):
+            nc.sync.dma_start(out=ws_raw[:, 1, t, :], in_=ws_view[1, t])
         ws_sc = [held.tile([P, N], U8, name="ws_sc%d" % b, align_bytes=64) for b in range(2)]
         HALF = PICKS // 2
-        z_pairs = [held.tile([P, 2, 2, HALF, 2], BF16, name="z_pairs%d" % b, align_bytes=64) for b in range(2)]
-        z_il0 = held.tile([P, HALF, PACK], BF16, name="z_il0", align_bytes=64)
+        z_pairs = [held.tile([P, 2, 2, HALF, 2], BF16, name="z_pairs0", align_bytes=64)]
+        z_il0 = held.tile([P, PICKS, PACK], BF16, name="z_il0", align_bytes=64)
         z_codes = [held.tile([P, PICKS], U32, name="z_codes%d" % b, align_bytes=64) for b in range(2)]
         z_sc = [held.tile([P, PICKS], U8, name="z_sc%d" % b, align_bytes=64) for b in range(2)]
 
         def interleave(copy, dst, src):
             copy(dst.rearrange("p (c i) t -> p c t i", i=4), src.rearrange("p t (c i) -> p c t i", i=4))
 
-        def weave(copy, dst, b, half):
+        def weave(copy, dst, b, half, cs=slice(0, HALF)):
             copy(
                 dst.rearrange("p c t -> p (c t)").bitcast(U32).rearrange("p (c u) -> p c u", u=2),
-                z_pairs[b][:, half].rearrange("p u c e -> p u (c e)").bitcast(U32).rearrange("p u c -> p c u"),
+                z_pairs[b][:, half].rearrange("p u c e -> p u (c e)").bitcast(U32)[:, :, cs].rearrange("p u c -> p c u"),
             )
 
         def quantize(codes, scales, il):
@@ -222,7 +222,7 @@ def tile_list_wildfire_layer_cession_kernel(
             b, t = place(i)
             dst = z_pairs[b][:, c0 // HALF : c1 // HALF, t // 2, :, t % 2]
             src = layered.rearrange("p (h c) -> p h c", c=HALF)
-            if i == 4:
+            if i in (3, 4):
                 nc.gpsimd.tensor_scalar(dst, src, term(2, i), 0.0, ALU.mult, ALU.add)
             else:
                 nc.scalar.activation(dst, src, ACT.Copy, scale=term(2, i))
@@ -232,7 +232,7 @@ def tile_list_wildfire_layer_cession_kernel(
 
         def second_product(b, half):
             for j in range(N // P):
-                if b == 0 and (half == 0 or j < 2):
+                if b == 0 and half == 0:
                     acc[j, half] = psum_o.tile([P, HALF], F32, name="acc%d%d" % (j, half))
                 elif b == 0:
                     acc[j, half] = psum_h.tile([P, BANK], F32, name="h_bank")
@@ -273,7 +273,7 @@ def tile_list_wildfire_layer_cession_kernel(
             for u in range((c1 - c0) // P):
                 ws_block[b, c0 // P + u] = codes[:, u * P : (u + 1) * P]
 
-        warm = psum_o.tile([P, BANK], F32, name="acc01")
+        warm = psum_o.tile([P, BANK], F32, name="acc20")
         for k in range(4):
             nc.tensor.matmul_mx(
                 out=warm[:],
@@ -351,47 +351,56 @@ def tile_list_wildfire_layer_cession_kernel(
             if k < 2:
                 round_ws(k + 1, "limit%d" % a)
             else:
+                z_pairs.append(one.tile([P, 2, 2, HALF, 2], BF16, name="z_pairs1", tag="limit%d" % a, align_bytes=64))
                 money(a, layered[a], 0, PICKS)
+                money(b - 2, layered[b - 2], 0, PICKS)
             first_product(a + 2)
-            lift_by_excess(b)
             first_product(b + 2)
+            lift_by_excess(b)
         pick_attach(last - 1)
         pick_limit(last - 1)
         pick_attach(last)
         pick_limit(last)
         pick_loss(last - 1)
         lift_whole(last - 1)
-        money(last - 4, layered[last - 4], 0, PICKS)
         cap_whole(last - 2)
         pick_loss(last)
-        weave(nc.scalar.copy, z_il0[:], 0, 0)
+        for half in range(2):
+            weave(nc.scalar.copy, z_il0[:, halves[half], :], 0, half)
         money(last - 2, layered[last - 2], 0, PICKS)
         lift_whole(last)
-        lay6 = windows[last % WINDOWS][:, S : S + PICKS]
-        cap(lay6, last - 1, limit[last - 1][:], lifted[last - 1][:])
-        quantize(z_codes[0][:, first], z_sc[0][:, first], z_il0[:])
+        quantize(z_codes[0][:, first], z_sc[0][:, first], z_il0[:, first, :])
         second_product(0, 0)
+        lay6 = windows[last % WINDOWS][:, S : S + PICKS]
         lay7 = lay_bufs[0]
+        cap(lay6[:, first], last - 1, limit[last - 1][:, first], lifted[last - 1][:, first])
         cap(lay7[:, first], last, limit[last][:, first], lifted[last][:, first])
+        cap(lay6[:, second], last - 1, limit[last - 1][:, second], lifted[last - 1][:, second])
+        quantize(z_codes[0][:, second], z_sc[0][:, second], z_il0[:, second, :])
+        second_product(0, 1)
         money(last - 1, lay6[:, first], 0, HALF)
         money(last, lay7[:, first], 0, HALF)
         z_il1 = [held.tile([P, HALF, PACK], BF16, name="z_il1%d" % half, align_bytes=64) for half in range(2)]
         weave(nc.scalar.copy, z_il1[0][:], 1, 0)
-        late_attach, late_limit = limit[last - 1][:, first], limit[last - 1][:, second]
-        pick(late_attach, last, pos2_t, HALF, PICKS)
-        pick(late_limit, last, pos3_t, HALF, PICKS)
         money(last - 1, lay6[:, second], HALF, PICKS)
-        z_il0_late = z_pairs[1][:, 0].rearrange("p u c e -> p (u c e)").rearrange("p (c t) -> p c t", t=PACK)
-        weave(nc.scalar.copy, z_il0_late, 0, 1)
-        lift(lay7[:, first], last, late_attach, HALF, PICKS)
+        late_attach = limit[last - 1][:, first]
+        pick(late_attach, last, pos2_t, HALF, PICKS)
         quantize(z_codes[1][:, first], z_sc[1][:, first], z_il1[0][:])
         second_product(1, 0)
-        cap(lay7[:, second], last, late_limit, lay7[:, first])
-        quantize(z_codes[0][:, second], z_sc[0][:, second], z_il0_late)
-        second_product(0, 1)
-        nc.vector.tensor_scalar(z_pairs[1][:, 1, 1, :, 1], lay7[:, second], term(2, last), None, ALU.mult)
+        late_limit = z_il1[0][:].rearrange("p c t -> p (c t)").bitcast(F32)[:, first]
+        pick(late_limit, last, pos3_t, HALF, PICKS)
+        quarters = [slice(q * P, (q + 1) * P) for q in range(2)]
+        late_lifted = lifted[last][:, second]
+        for q, cs in enumerate(quarters):
+            lift(late_lifted[:, cs], last, late_attach[:, cs], HALF + q * P, HALF + (q + 1) * P)
+        for cs in quarters:
+            cap(lay7[:, second][:, cs], last, late_limit[:, cs], late_lifted[:, cs])
+        for cs in quarters:
+            nc.vector.tensor_scalar(z_pairs[1][:, 1, 1, cs, 1], lay7[:, second][:, cs], term(2, last), None, ALU.mult)
         store(0)
-        weave(nc.vector.tensor_copy, z_il1[1][:], 1, 1)
-        quantize(z_codes[1][:, second], z_sc[1][:, second], z_il1[1][:])
+        for cs in quarters:
+            weave(nc.vector.tensor_copy, z_il1[1][:, cs, :], 1, 1, cs)
+        for cs in quarters:
+            quantize(z_codes[1][:, second][:, cs], z_sc[1][:, second][:, cs], z_il1[1][:, cs, :])
         second_product(1, 1)
         store(1)

@@ -84,7 +84,7 @@ def tile_list_wildfire_layer_cession_kernel(
         terms = held.tile([P, PACK, 6], F32, name="terms")
 
         def place(i):
-            return ((0, 2), (0, 0), (0, 1), (1, 2), (0, 3), (1, 0), (1, 1), (1, 3))[i]
+            return i // PACK, (2, 0, 1, 3)[i % PACK]
 
         def term(v, i):
             b, t = place(i)
@@ -145,7 +145,7 @@ def tile_list_wildfire_layer_cession_kernel(
             nc.sync.dma_start(out=ws_raw[:, 1, t, :], in_=ws_view[1, t])
         ws_sc = [held.tile([P, N], U8, name="ws_sc%d" % b, align_bytes=64) for b in range(2)]
         HALF = PICKS // 2
-        z_pairs = [held.tile([P, 2, 2, HALF, 2], BF16, name="z_pairs0", align_bytes=64)]
+        z_pairs = [held.tile([P, 2, 2, HALF, 2], BF16, name="z_pairs%d" % b, align_bytes=64) for b in range(2)]
         z_il0 = held.tile([P, PICKS, PACK], BF16, name="z_il0", align_bytes=64)
         z_codes = [held.tile([P, PICKS], U32, name="z_codes%d" % b, align_bytes=64) for b in range(2)]
         z_sc = [held.tile([P, PICKS], U8, name="z_sc%d" % b, align_bytes=64) for b in range(2)]
@@ -222,8 +222,8 @@ def tile_list_wildfire_layer_cession_kernel(
             b, t = place(i)
             dst = z_pairs[b][:, c0 // HALF : c1 // HALF, t // 2, :, t % 2]
             src = layered.rearrange("p (h c) -> p h c", c=HALF)
-            if i in (3, 4):
-                nc.gpsimd.tensor_scalar(dst, src, term(2, i), 0.0, ALU.mult, ALU.add)
+            if i == 4:
+                nc.gpsimd.tensor_tensor(dst, src, term(2, i).unsqueeze(1).to_broadcast([P, 2, HALF]), ALU.mult)
             else:
                 nc.scalar.activation(dst, src, ACT.Copy, scale=term(2, i))
 
@@ -351,9 +351,7 @@ def tile_list_wildfire_layer_cession_kernel(
             if k < 2:
                 round_ws(k + 1, "limit%d" % a)
             else:
-                z_pairs.append(one.tile([P, 2, 2, HALF, 2], BF16, name="z_pairs1", tag="limit%d" % a, align_bytes=64))
                 money(a, layered[a], 0, PICKS)
-                money(b - 2, layered[b - 2], 0, PICKS)
             first_product(a + 2)
             first_product(b + 2)
             lift_by_excess(b)
@@ -363,6 +361,7 @@ def tile_list_wildfire_layer_cession_kernel(
         pick_limit(last)
         pick_loss(last - 1)
         lift_whole(last - 1)
+        money(last - 4, layered[last - 4], 0, PICKS)
         cap_whole(last - 2)
         pick_loss(last)
         for half in range(2):
@@ -371,26 +370,26 @@ def tile_list_wildfire_layer_cession_kernel(
         lift_whole(last)
         quantize(z_codes[0][:, first], z_sc[0][:, first], z_il0[:, first, :])
         second_product(0, 0)
-        lay6 = windows[last % WINDOWS][:, S : S + PICKS]
+        lay6 = windows[last % WINDOWS][:, S : S + HALF]
         lay7 = lay_bufs[0]
-        cap(lay6[:, first], last - 1, limit[last - 1][:, first], lifted[last - 1][:, first])
+        cap(lay6, last - 1, limit[last - 1][:, first], lifted[last - 1][:, first])
         cap(lay7[:, first], last, limit[last][:, first], lifted[last][:, first])
-        cap(lay6[:, second], last - 1, limit[last - 1][:, second], lifted[last - 1][:, second])
         quantize(z_codes[0][:, second], z_sc[0][:, second], z_il0[:, second, :])
         second_product(0, 1)
-        money(last - 1, lay6[:, first], 0, HALF)
+        money(last - 1, lay6, 0, HALF)
         money(last, lay7[:, first], 0, HALF)
         z_il1 = [held.tile([P, HALF, PACK], BF16, name="z_il1%d" % half, align_bytes=64) for half in range(2)]
         weave(nc.scalar.copy, z_il1[0][:], 1, 0)
-        money(last - 1, lay6[:, second], HALF, PICKS)
-        late_attach = limit[last - 1][:, first]
+        late_attach, late_limit = limit[last - 1][:, first], limit[last][:, first]
         pick(late_attach, last, pos2_t, HALF, PICKS)
+        pick(late_limit, last, pos3_t, HALF, PICKS)
         quantize(z_codes[1][:, first], z_sc[1][:, first], z_il1[0][:])
         second_product(1, 0)
-        late_limit = z_il1[0][:].rearrange("p c t -> p (c t)").bitcast(F32)[:, first]
-        pick(late_limit, last, pos3_t, HALF, PICKS)
+        late_lay6 = z_pairs[1][:, 0].rearrange("p u c e -> p (u c e)").bitcast(F32)[:, first]
+        cap(late_lay6, last - 1, limit[last - 1][:, second], lifted[last - 1][:, second])
+        money(last - 1, late_lay6, HALF, PICKS)
         quarters = [slice(q * P, (q + 1) * P) for q in range(2)]
-        late_lifted = lifted[last][:, second]
+        late_lifted = z_il1[0][:].rearrange("p c t -> p (c t)").bitcast(F32)[:, first]
         for q, cs in enumerate(quarters):
             lift(late_lifted[:, cs], last, late_attach[:, cs], HALF + q * P, HALF + (q + 1) * P)
         for cs in quarters:

@@ -223,7 +223,7 @@ def tile_list_wildfire_layer_cession_kernel(
             dst = z_pairs[b][:, c0 // HALF : c1 // HALF, t // 2, :, t % 2]
             src = layered.rearrange("p (h c) -> p h c", c=HALF)
             if i == 4:
-                nc.gpsimd.tensor_tensor(dst, src, term(2, i).unsqueeze(1).to_broadcast([P, 2, HALF]), ALU.mult)
+                nc.gpsimd.tensor_scalar(dst, src, term(2, i), 0.0, ALU.mult, ALU.add)
             else:
                 nc.scalar.activation(dst, src, ACT.Copy, scale=term(2, i))
 
@@ -337,11 +337,17 @@ def tile_list_wildfire_layer_cession_kernel(
             pick_attach(a)
             pick_limit(a)
             pick_limit(b)
-            pick_loss(a)
-            pick_loss(b)
-            lift_whole(a)
-            pick_excess(b)
-            quantize_ws(k, "attach%d" % a)
+            if k == 0:
+                pick_loss(b)
+                pick_loss(a)
+                pick_excess(b)
+                lift_whole(a)
+            else:
+                pick_loss(a)
+                pick_loss(b)
+                lift_whole(a)
+                pick_excess(b)
+                quantize_ws(k - 1, "attach%d" % a)
             if k >= 2:
                 money(b - 4, layered[b - 4], 0, PICKS)
             if k >= 1:
@@ -361,6 +367,7 @@ def tile_list_wildfire_layer_cession_kernel(
         pick_limit(last)
         pick_loss(last - 1)
         lift_whole(last - 1)
+        quantize_ws(2, "attach%d" % (last - 1))
         money(last - 4, layered[last - 4], 0, PICKS)
         cap_whole(last - 2)
         pick_loss(last)

@@ -222,10 +222,7 @@ def tile_list_wildfire_layer_cession_kernel(
             b, t = place(i)
             dst = z_pairs[b][:, c0 // HALF : c1 // HALF, t // 2, :, t % 2]
             src = layered.rearrange("p (h c) -> p h c", c=HALF)
-            if i == 4:
-                nc.gpsimd.tensor_scalar(dst, src, term(2, i), 0.0, ALU.mult, ALU.add)
-            else:
-                nc.scalar.activation(dst, src, ACT.Copy, scale=term(2, i))
+            nc.scalar.activation(dst, src, ACT.Copy, scale=term(2, i))
 
         acc = {}
         ws_block = {}
@@ -258,20 +255,29 @@ def tile_list_wildfire_layer_cession_kernel(
                 )
 
         ws_il = {}
-        ws_parts = ((0, 0, N), (1, 0, N // 2), (1, N // 2, N))
+        ws_parts = ((0, 0, 3), (0, 3, 4), (1, 0, 2), (1, 2, 4))
 
         def round_ws(k, tag):
-            b, c0, c1 = ws_parts[k]
-            ws_il[k] = one.tile([P, c1 - c0, PACK], BF16, name="ws_il%d" % k, tag=tag, align_bytes=64)
-            src = ws_raw[:, b, :, c0:c1]
+            b, j0, j1 = ws_parts[k]
+            ws_il[k] = one.tile([P, (j1 - j0) * P, PACK], BF16, name="ws_il%d" % k, tag=tag, align_bytes=64)
+            src = ws_raw[:, b, :, j0 * P : j1 * P]
             nc.gpsimd.tensor_scalar(ws_il[k][:], src.rearrange("p t n -> p n t"), 1.0, 0.0, ALU.mult, ALU.add)
 
-        def quantize_ws(k, tag):
-            b, c0, c1 = ws_parts[k]
-            codes = one.tile([P, c1 - c0], U32, name="ws_codes%d" % k, tag=tag, align_bytes=64)
-            quantize(codes[:], ws_sc[b][:, c0:c1], ws_il[k][:])
-            for u in range((c1 - c0) // P):
-                ws_block[b, c0 // P + u] = codes[:, u * P : (u + 1) * P]
+        def quantize_ws(parts, tag):
+            first_block = ws_parts[parts[0]][1]
+            width = (ws_parts[parts[-1]][2] - first_block) * P
+            codes = one.tile([P, width], U32, name="ws_codes%d" % parts[0], tag=tag, align_bytes=64)
+            for k in parts:
+                b, j0, j1 = ws_parts[k]
+                for j in range(j0, j1, 2):
+                    end = min(j + 2, j1)
+                    quantize(
+                        codes[:, (j - first_block) * P : (end - first_block) * P],
+                        ws_sc[b][:, j * P : end * P],
+                        ws_il[k][:, (j - j0) * P : (end - j0) * P, :],
+                    )
+                for j in range(j0, j1):
+                    ws_block[b, j] = codes[:, (j - first_block) * P : (j - first_block + 1) * P]
 
         warm = psum_o.tile([P, BANK], F32, name="acc20")
         for k in range(4):
@@ -310,7 +316,7 @@ def tile_list_wildfire_layer_cession_kernel(
         lay_bufs = [held.tile([P, PICKS], F32, name="lay_buf%d" % k) for k in range(2)]
 
         def lift_whole(i):
-            lifted[i] = lift_bufs[2 if i == last else i // 2 % 2]
+            lifted[i] = lift_bufs[2 if i % 2 else i // 2 % 2]
             end = HALF if i == last else PICKS
             lift(lifted[i][:, 0:end], i, attach[i][:, 0:end], 0, end)
 
@@ -336,6 +342,8 @@ def tile_list_wildfire_layer_cession_kernel(
             a, b = 2 * k, 2 * k + 1
             pick_attach(a)
             pick_limit(a)
+            if k == 2:
+                pick_attach(b)
             pick_limit(b)
             if k == 0:
                 pick_loss(b)
@@ -346,29 +354,31 @@ def tile_list_wildfire_layer_cession_kernel(
                 pick_loss(a)
                 pick_loss(b)
                 lift_whole(a)
-                pick_excess(b)
-                quantize_ws(k - 1, "attach%d" % a)
+                if k == 2:
+                    lift_whole(b)
+                else:
+                    pick_excess(b)
+                quantize_ws((k - 1,), "attach%d" % a)
             if k >= 2:
                 money(b - 4, layered[b - 4], 0, PICKS)
             if k >= 1:
                 cap_whole(b - 2)
                 money(a - 2, layered[a - 2], 0, PICKS)
             cap_whole(a)
-            if k < 2:
-                round_ws(k + 1, "limit%d" % a)
-            else:
-                money(a, layered[a], 0, PICKS)
+            round_ws(k + 1, "limit%d" % a)
             first_product(a + 2)
             first_product(b + 2)
-            lift_by_excess(b)
+            if k < 2:
+                lift_by_excess(b)
         pick_attach(last - 1)
         pick_limit(last - 1)
         pick_attach(last)
         pick_limit(last)
         pick_loss(last - 1)
         lift_whole(last - 1)
-        quantize_ws(2, "attach%d" % (last - 1))
+        quantize_ws((2, 3), "attach%d" % (last - 1))
         money(last - 4, layered[last - 4], 0, PICKS)
+        money(last - 3, layered[last - 3], 0, PICKS)
         cap_whole(last - 2)
         pick_loss(last)
         for half in range(2):

@@ -24,6 +24,9 @@ BANK = 512
 WINDOW = 2048
 WINDOWS = 4
 SLICES = H // P
+HALF = PICKS // 2
+EARLY = S + PASS
+QUADRANTS = (0, 2, 1, 3)
 
 
 def tile_list_wildfire_layer_cession_kernel(
@@ -70,7 +73,6 @@ def tile_list_wildfire_layer_cession_kernel(
         for raw in (w4_sc_raw, tab_sc):
             nc.vector.memset(raw[32:64, :], 0)
             nc.vector.memset(raw[64:128, :], 0)
-        EARLY = S + PASS
         planes_early = held.tile([P, 2, EARLY // 4], I32, name="planes_early", align_bytes=64)
         nc.gpsimd.memset(planes_early[:], 0)
 
@@ -82,6 +84,7 @@ def tile_list_wildfire_layer_cession_kernel(
         make_identity(nc, ident[:])
         term_rows = held.tile([P, PACK, P], F32, name="term_rows")
         terms = held.tile([P, PACK, 6], F32, name="terms")
+        ATT, LIM, GAIN = range(3)
 
         def place(i):
             return i // PACK, (2, 0, 1, 3)[i % PACK]
@@ -97,13 +100,14 @@ def tile_list_wildfire_layer_cession_kernel(
             windows.append(win)
 
         nc.scalar.copy(
-            term_rows[:].rearrange("p t (g q) -> p t g q", q=8), term_raw[:].rearrange("p (g t q) -> p t g q", t=PACK, q=8)
+            term_rows[:].rearrange("p t (g q) -> p t g q", q=8),
+            term_raw[:].rearrange("p (g t q) -> p t g q", t=PACK, q=8),
         )
 
         rows = held.tile([P, (S + H) // 4], I32, name="rows", align_bytes=64)
         nc.vector.tensor_copy(
-            out=rows[:, S // 4 :].rearrange("p (b t g k) -> p b t g k", b=2, t=PACK, k=2),
-            in_=w4_sc_raw[:].rearrange("p (b g t k) -> p b t g k", b=2, t=PACK, k=2),
+            out=rows[:, S // 4 :].rearrange("p (b t g x) -> p b t g x", b=2, t=PACK, x=2),
+            in_=w4_sc_raw[:].rearrange("p (b g t x) -> p b t g x", b=2, t=PACK, x=2),
         )
         v_sc_rows = one.tile([P, S], U8, name="v_sc_rows", tag="late", align_bytes=64)
         nc.vector.tensor_copy(v_sc_rows[:], tab_sc[:].bitcast(U8).indirect(offs_t[:]))
@@ -111,13 +115,16 @@ def tile_list_wildfire_layer_cession_kernel(
 
         def order_columns(b, raw):
             nc.vector.tensor_copy(
-                out=w4_codes[b][:].rearrange("p a (t g k) -> p a t g k", t=PACK, k=4),
-                in_=raw[:].rearrange("p a (g t k) -> p a t g k", t=PACK, k=4),
+                out=w4_codes[b][:].rearrange("p a (t g x) -> p a t g x", t=PACK, x=4),
+                in_=raw[:].rearrange("p a (g t x) -> p a t g x", t=PACK, x=4),
             )
 
+        def move_rows(planes, words):
+            for quad in QUADRANTS:
+                nc.sync.dma_start(out=planes[32 * quad : 32 * quad + 4, :, :], in_=rows[8 * quad : 8 * quad + 8, words])
+
         nc.vector.tensor_copy(rows[:, 0 : S // 4], v_sc_rows[:].bitcast(I32))
-        for q in (0, 2, 1, 3):
-            nc.sync.dma_start(out=planes_early[32 * q : 32 * q + 4, :, :], in_=rows[8 * q : 8 * q + 8, 0 : EARLY // 4])
+        move_rows(planes_early, slice(0, EARLY // 4))
         w4_raw1 = one.tile([P, 2, H // 4], I32, name="w4_raw1", tag="late", align_bytes=64)
         nc.sync.dma_start(out=w4_raw1[:], in_=w4_view[:, :, H // 4 : H // 2])
         order_columns(0, w4_raw0)
@@ -128,7 +135,7 @@ def tile_list_wildfire_layer_cession_kernel(
             for half in range(2):
                 nc.vector.tensor_copy(
                     codes[:, half * BANK : (half + 1) * BANK],
-                    tab_w[a][:].bitcast(U32).indirect(offs_t[:, half * 32 : (half + 1) * 32]),
+                    tab_w[a][:].bitcast(U32).indirect(offs_t[:, half * BANK // 16 : (half + 1) * BANK // 16]),
                 )
             v_codes.append(codes)
         order_columns(1, w4_raw1)
@@ -139,30 +146,26 @@ def tile_list_wildfire_layer_cession_kernel(
             nc.sync.dma_start(out=ws_raw[:, 0, t, :], in_=ws_view[0, t])
         planes_late = one.tile([P, 2, PASS // 4], I32, name="planes_late", tag="big1", align_bytes=64)
         nc.gpsimd.memset(planes_late[:], 0)
-        for q in (0, 2, 1, 3):
-            nc.sync.dma_start(out=planes_late[32 * q : 32 * q + 4, :, :], in_=rows[8 * q : 8 * q + 8, EARLY // 4 :])
+        move_rows(planes_late, slice(EARLY // 4, (S + H) // 4))
         for t in range(PACK):
             nc.sync.dma_start(out=ws_raw[:, 1, t, :], in_=ws_view[1, t])
         ws_sc = [held.tile([P, N], U8, name="ws_sc%d" % b, align_bytes=64) for b in range(2)]
-        HALF = PICKS // 2
         z_pairs = [held.tile([P, 2, 2, HALF, 2], BF16, name="z_pairs%d" % b, align_bytes=64) for b in range(2)]
         z_il0 = held.tile([P, PICKS, PACK], BF16, name="z_il0", align_bytes=64)
         z_codes = [held.tile([P, PICKS], U32, name="z_codes%d" % b, align_bytes=64) for b in range(2)]
         z_sc = [held.tile([P, PICKS], U8, name="z_sc%d" % b, align_bytes=64) for b in range(2)]
 
-        def interleave(copy, dst, src):
-            copy(dst.rearrange("p (c i) t -> p c t i", i=4), src.rearrange("p t (c i) -> p c t i", i=4))
-
-        def weave(copy, dst, b, half, cs=slice(0, HALF)):
+        def weave(copy, dst, b, half, cols):
+            pairs = z_pairs[b][:, half].rearrange("p u c e -> p u (c e)").bitcast(U32)
             copy(
                 dst.rearrange("p c t -> p (c t)").bitcast(U32).rearrange("p (c u) -> p c u", u=2),
-                z_pairs[b][:, half].rearrange("p u c e -> p u (c e)").bitcast(U32)[:, :, cs].rearrange("p u c -> p c u"),
+                pairs[:, :, cols].rearrange("p u c -> p c u"),
             )
 
         def quantize(codes, scales, il):
             nc.vector.quantize_mx(out=codes.bitcast(FP8X4), scales=scales, in_=il.rearrange("p n t -> p (n t)"))
 
-        def h_pass(i, a, dst, c0, c1, start, stop):
+        def h_pass(i, a, dst, c0, c1):
             b, t = place(i)
             if b == 0:
                 w4_plane = planes_early[:, a, :].bitcast(U8)[:, S + P * t : S + P * (t + 1)]
@@ -174,34 +177,28 @@ def tile_list_wildfire_layer_cession_kernel(
                 lhsT_scale=w4_plane,
                 rhs=v_codes[a][:, c0:c1].bitcast(FP8X4),
                 rhs_scale=planes_early[:, a, :].bitcast(U8)[:, c0:c1],
-                start=start,
-                stop=stop,
+                start=(a == 0),
+                stop=(a == 1),
             )
-
-        def h_bank(i, half):
-            bank = psum_h.tile([P, BANK], F32, name="h_bank")
-            for a in range(2):
-                h_pass(i, a, bank[:], half * BANK, (half + 1) * BANK, a == 0, a == 1)
-            nc.scalar.copy(windows[i % WINDOWS][:, half * BANK : (half + 1) * BANK], bank[:])
 
         def first_product(i):
             for half in range(2):
-                h_bank(i, half)
+                bank = psum_h.tile([P, BANK], F32, name="h_bank")
+                for a in range(2):
+                    h_pass(i, a, bank[:], half * BANK, (half + 1) * BANK)
+                nc.scalar.copy(windows[i % WINDOWS][:, half * BANK : (half + 1) * BANK], bank[:])
 
         def first_slice():
             banks = [psum_h.tile([P, BANK], F32, name="h_bank")]
-            banks += [psum_o.tile([P, HALF], F32, name="acc%d0" % q) for q in range(2)]
+            banks += [psum_o.tile([P, P], F32, name="acc%d0" % j) for j in range(4)]
             for a in range(2):
-                h_pass(0, a, banks[0][:], 0, BANK, a == 0, a == 1)
-                for q in range(2):
-                    for u in range(2):
-                        c0 = BANK + q * HALF + u * P
-                        h_pass(
-                            0, a, banks[1 + q][:, u * P : (u + 1) * P], c0, c0 + P, a == 0 and u == 0, a == 1 and u == 1
-                        )
+                h_pass(0, a, banks[0][:], 0, BANK)
+                for j in range(4):
+                    h_pass(0, a, banks[1 + j][:], BANK + j * P, BANK + (j + 1) * P)
             nc.scalar.copy(windows[0][:, 0:BANK], banks[0][:])
-            for q, copy in enumerate((nc.vector.tensor_copy, nc.scalar.copy)):
-                copy(windows[0][:, BANK + q * HALF : BANK + (q + 1) * HALF], banks[1 + q][:, 0:HALF])
+            for j in range(4):
+                copy = (nc.vector.tensor_copy, nc.scalar.copy)[j % 2]
+                copy(windows[0][:, BANK + j * P : BANK + (j + 1) * P], banks[1 + j][:])
 
         loss = {}
 
@@ -212,17 +209,20 @@ def tile_list_wildfire_layer_cession_kernel(
         def pick(dst, i, pos_t, c0, c1):
             nc.vector.tensor_copy(dst, windows[i % WINDOWS][:, 0:S].indirect(pos_t[:, c0 // 16 : c1 // 16]))
 
-        def lift(dst, i, attach, c0, c1):
-            nc.vector.scalar_tensor_tensor(dst, attach, term(0, i), loss[i][:, c0:c1], ALU.add, ALU.max)
+        def lift(dst, i, picked, c0, c1):
+            nc.vector.scalar_tensor_tensor(dst, picked, term(ATT, i), loss[i][:, c0:c1], ALU.add, ALU.max)
 
-        def cap(dst, i, limit, lifted):
-            nc.vector.scalar_tensor_tensor(dst, limit, term(1, i), lifted, ALU.add, ALU.min)
+        def cap(dst, i, picked, lifted_loss):
+            nc.vector.scalar_tensor_tensor(dst, picked, term(LIM, i), lifted_loss, ALU.add, ALU.min)
 
-        def money(i, layered, c0, c1):
+        def money(i, src, c0, c1):
             b, t = place(i)
             dst = z_pairs[b][:, c0 // HALF : c1 // HALF, t // 2, :, t % 2]
-            src = layered.rearrange("p (h c) -> p h c", c=HALF)
-            nc.scalar.activation(dst, src, ACT.Copy, scale=term(2, i))
+            nc.scalar.activation(dst, src.rearrange("p (h c) -> p h c", c=HALF), ACT.Copy, scale=term(GAIN, i))
+
+        def late_money(i, src, cols):
+            b, t = place(i)
+            nc.vector.tensor_scalar(z_pairs[b][:, 1, t // 2, cols, t % 2], src, term(GAIN, i), None, ALU.mult)
 
         acc = {}
         ws_block = {}
@@ -245,42 +245,42 @@ def tile_list_wildfire_layer_cession_kernel(
 
         out_view = out.rearrange("(j p) m -> p j m", p=P)
 
-        def store(half):
+        def store(half, copies):
             for pair in range(2):
                 res = held.tile([P, 2, HALF], F32, name="res%d%d" % (pair, half))
-                for u, copy in enumerate((nc.scalar.copy, (nc.scalar.copy, nc.vector.tensor_copy)[half])):
+                for u, copy in enumerate(copies):
                     copy(res[:, u, :], acc[2 * pair + u, half][:, 0:HALF])
                 nc.sync.dma_start(
                     out=out_view[:, 2 * pair : 2 * pair + 2, half * HALF : (half + 1) * HALF], in_=res[:]
                 )
 
         ws_il = {}
-        ws_parts = ((0, 0, 3), (0, 3, 4), (1, 0, 2), (1, 2, 4))
 
-        def round_ws(k, tag):
-            b, j0, j1 = ws_parts[k]
-            ws_il[k] = one.tile([P, (j1 - j0) * P, PACK], BF16, name="ws_il%d" % k, tag=tag, align_bytes=64)
-            src = ws_raw[:, b, :, j0 * P : j1 * P]
-            nc.gpsimd.tensor_scalar(ws_il[k][:], src.rearrange("p t n -> p n t"), 1.0, 0.0, ALU.mult, ALU.add)
+        def ws_rows(piece, cols):
+            b, s = divmod(piece, 2)
+            return ws_raw[:, b, :, s * HALF : (s + 1) * HALF][:, :, cols]
 
-        def quantize_ws(parts, tag):
-            first_block = ws_parts[parts[0]][1]
-            width = (ws_parts[parts[-1]][2] - first_block) * P
-            codes = one.tile([P, width], U32, name="ws_codes%d" % parts[0], tag=tag, align_bytes=64)
-            for k in parts:
-                b, j0, j1 = ws_parts[k]
-                for j in range(j0, j1, 2):
-                    end = min(j + 2, j1)
-                    quantize(
-                        codes[:, (j - first_block) * P : (end - first_block) * P],
-                        ws_sc[b][:, j * P : end * P],
-                        ws_il[k][:, (j - j0) * P : (end - j0) * P, :],
-                    )
-                for j in range(j0, j1):
-                    ws_block[b, j] = codes[:, (j - first_block) * P : (j - first_block + 1) * P]
+        def round_ws(piece, tag, cols):
+            ws_il[piece] = one.tile([P, HALF, PACK], BF16, name="ws_il%d" % piece, tag=tag, align_bytes=64)
+            src = ws_rows(piece, cols).rearrange("p t n -> p n t")
+            nc.gpsimd.tensor_scalar(ws_il[piece][:, cols, :], src, 1.0, 0.0, ALU.mult, ALU.add)
+
+        def round_ws_on_scalar(piece, cols):
+            nc.scalar.copy(
+                ws_il[piece][:, cols, :].rearrange("p (c x) t -> p c t x", x=4),
+                ws_rows(piece, cols).rearrange("p t (c x) -> p c t x", x=4),
+            )
+
+        def quantize_ws(pieces, tag):
+            codes = one.tile([P, len(pieces), HALF], U32, name="ws_codes%d" % pieces[0], tag=tag, align_bytes=64)
+            for n, piece in enumerate(pieces):
+                b, s = divmod(piece, 2)
+                quantize(codes[:, n, :], ws_sc[b][:, s * HALF : (s + 1) * HALF], ws_il[piece][:])
+                for u in range(2):
+                    ws_block[b, 2 * s + u] = codes[:, n, u * P : (u + 1) * P]
 
         warm = psum_o.tile([P, BANK], F32, name="acc20")
-        for k in range(4):
+        for turn in range(4):
             nc.tensor.matmul_mx(
                 out=warm[:],
                 lhsT=w4_codes[0][:, 0, :].bitcast(U8)[:, 0 : 2 * P].bitcast(FP4X4),
@@ -297,30 +297,27 @@ def tile_list_wildfire_layer_cession_kernel(
             nc.tensor.transpose(turned[:, t * P : (t + 1) * P], term_rows[:, t, :], ident[:])
         nc.scalar.copy(terms[:], turned[:].rearrange("p (t j) -> p t j", t=PACK)[:, :, 0:6])
 
-
-        attach, limit, lifted, layered = {}, {}, {}, {}
+        attach, limit, excess, lifted, layered = {}, {}, {}, {}, {}
         last = SLICES - 1
-        halves = [slice(half * HALF, (half + 1) * HALF) for half in range(2)]
+        first, second = slice(0, HALF), slice(HALF, PICKS)
+
+        def width(i):
+            return HALF if i == last else PICKS
 
         def pick_attach(i):
             attach[i] = one.tile([P, PICKS], F32, name="attach%d" % i, tag="attach%d" % i, align_bytes=64)
-            end = HALF if i == last else PICKS
-            pick(attach[i][:, 0:end], i, pos2_t, 0, end)
+            pick(attach[i][:, 0 : width(i)], i, pos2_t, 0, width(i))
 
         def pick_limit(i):
             limit[i] = one.tile([P, PICKS], F32, name="limit%d" % i, tag="limit%d" % i, align_bytes=64)
-            end = HALF if i == last else PICKS
-            pick(limit[i][:, 0:end], i, pos3_t, 0, end)
+            pick(limit[i][:, 0 : width(i)], i, pos3_t, 0, width(i))
 
-        lift_bufs = [held.tile([P, PICKS], F32, name="lift_buf%d" % k) for k in range(3)]
-        lay_bufs = [held.tile([P, PICKS], F32, name="lay_buf%d" % k) for k in range(2)]
+        lift_bufs = [held.tile([P, PICKS], F32, name="lift_buf%d" % n) for n in range(3)]
+        lay_bufs = [held.tile([P, PICKS], F32, name="lay_buf%d" % n) for n in range(2)]
 
-        def lift_whole(i):
+        def lift_slice(i):
             lifted[i] = lift_bufs[2 if i % 2 else i // 2 % 2]
-            end = HALF if i == last else PICKS
-            lift(lifted[i][:, 0:end], i, attach[i][:, 0:end], 0, end)
-
-        excess = {}
+            lift(lifted[i][:, 0 : width(i)], i, attach[i][:, 0 : width(i)], 0, width(i))
 
         def pick_excess(i):
             excess[i] = ring.tile([P, PICKS], F32, name="excess", bufs=2)
@@ -328,95 +325,114 @@ def tile_list_wildfire_layer_cession_kernel(
 
         def lift_by_excess(i):
             rise = ring.tile([P, PICKS], F32, name="rise", bufs=2)
-            nc.scalar.activation(rise[:], excess[i][:], ACT.Relu, bias=term(0, i))
+            nc.scalar.activation(rise[:], excess[i][:], ACT.Relu, bias=term(ATT, i))
             lifted[i] = lift_bufs[i // 2 % 2]
             nc.gpsimd.tensor_tensor(lifted[i][:], loss[i][:], rise[:], ALU.add)
 
-        def cap_whole(i):
+        def cap_slice(i):
             layered[i] = lay_bufs[i % 2][:, :]
             cap(layered[i], i, limit[i][:], lifted[i][:])
 
-        first, second = halves
-        round_ws(0, "ws_il0")
-        for k in range(3):
-            a, b = 2 * k, 2 * k + 1
-            pick_attach(a)
-            pick_limit(a)
-            if k == 2:
-                pick_attach(b)
-            pick_limit(b)
-            if k == 0:
-                pick_loss(b)
-                pick_loss(a)
-                pick_excess(b)
-                lift_whole(a)
-            else:
-                pick_loss(a)
-                pick_loss(b)
-                lift_whole(a)
-                if k == 2:
-                    lift_whole(b)
-                else:
-                    pick_excess(b)
-                quantize_ws((k - 1,), "attach%d" % a)
-            if k >= 2:
-                money(b - 4, layered[b - 4], 0, PICKS)
-            if k >= 1:
-                cap_whole(b - 2)
-                money(a - 2, layered[a - 2], 0, PICKS)
-            cap_whole(a)
-            round_ws(k + 1, "limit%d" % a)
-            first_product(a + 2)
-            first_product(b + 2)
-            if k < 2:
-                lift_by_excess(b)
-        pick_attach(last - 1)
-        pick_limit(last - 1)
-        pick_attach(last)
-        pick_limit(last)
-        pick_loss(last - 1)
-        lift_whole(last - 1)
-        quantize_ws((2, 3), "attach%d" % (last - 1))
-        money(last - 4, layered[last - 4], 0, PICKS)
-        money(last - 3, layered[last - 3], 0, PICKS)
-        cap_whole(last - 2)
-        pick_loss(last)
-        for half in range(2):
-            weave(nc.scalar.copy, z_il0[:, halves[half], :], 0, half)
-        money(last - 2, layered[last - 2], 0, PICKS)
-        lift_whole(last)
+        def money_slice(i):
+            money(i, layered[i], 0, PICKS)
+
+        def next_pair(even):
+            first_product(even + 2)
+            first_product(even + 3)
+
+        round_ws(0, "ws_il0", first)
+        pick_attach(0)
+        pick_limit(0)
+        pick_limit(1)
+        pick_loss(1)
+        pick_loss(0)
+        pick_excess(1)
+        lift_slice(0)
+        cap_slice(0)
+        round_ws(1, "limit0", slice(0, P))
+        next_pair(0)
+        lift_by_excess(1)
+
+        pick_attach(2)
+        pick_limit(2)
+        pick_limit(3)
+        pick_loss(2)
+        pick_loss(3)
+        lift_slice(2)
+        pick_excess(3)
+        quantize_ws((0,), "attach2")
+        cap_slice(1)
+        money_slice(0)
+        cap_slice(2)
+        round_ws(2, "limit2", first)
+        round_ws_on_scalar(1, slice(P, HALF))
+        next_pair(2)
+        lift_by_excess(3)
+
+        pick_attach(4)
+        pick_limit(4)
+        pick_attach(5)
+        pick_limit(5)
+        pick_loss(4)
+        pick_loss(5)
+        lift_slice(4)
+        lift_slice(5)
+        quantize_ws((1,), "attach4")
+        money_slice(1)
+        cap_slice(3)
+        money_slice(2)
+        cap_slice(4)
+        round_ws(3, "limit4", first)
+        next_pair(4)
+
+        pick_attach(6)
+        pick_limit(6)
+        pick_attach(7)
+        pick_limit(7)
+        pick_loss(6)
+        lift_slice(6)
+        quantize_ws((2, 3), "attach6")
+        money_slice(3)
+        money_slice(4)
+        cap_slice(5)
+        pick_loss(7)
+        weave(nc.scalar.copy, z_il0[:, first, :], 0, 0, first)
+        weave(nc.scalar.copy, z_il0[:, second, :], 0, 1, first)
+        money_slice(5)
+        lift_slice(7)
         quantize(z_codes[0][:, first], z_sc[0][:, first], z_il0[:, first, :])
         second_product(0, 0)
-        lay6 = windows[last % WINDOWS][:, S : S + HALF]
+        lay6 = windows[7 % WINDOWS][:, S : S + HALF]
         lay7 = lay_bufs[0]
-        cap(lay6, last - 1, limit[last - 1][:, first], lifted[last - 1][:, first])
-        cap(lay7[:, first], last, limit[last][:, first], lifted[last][:, first])
+        cap(lay6, 6, limit[6][:, first], lifted[6][:, first])
+        cap(lay7[:, first], 7, limit[7][:, first], lifted[7][:, first])
         quantize(z_codes[0][:, second], z_sc[0][:, second], z_il0[:, second, :])
         second_product(0, 1)
-        money(last - 1, lay6, 0, HALF)
-        money(last, lay7[:, first], 0, HALF)
+        money(6, lay6, 0, HALF)
+        money(7, lay7[:, first], 0, HALF)
         z_il1 = [held.tile([P, HALF, PACK], BF16, name="z_il1%d" % half, align_bytes=64) for half in range(2)]
-        weave(nc.scalar.copy, z_il1[0][:], 1, 0)
-        late_attach, late_limit = limit[last - 1][:, first], limit[last][:, first]
-        pick(late_attach, last, pos2_t, HALF, PICKS)
-        pick(late_limit, last, pos3_t, HALF, PICKS)
+        weave(nc.scalar.copy, z_il1[0][:], 1, 0, first)
+
+        late_attach, late_limit = limit[6][:, first], limit[7][:, first]
+        pick(late_attach, 7, pos2_t, HALF, PICKS)
+        pick(late_limit, 7, pos3_t, HALF, PICKS)
         quantize(z_codes[1][:, first], z_sc[1][:, first], z_il1[0][:])
         second_product(1, 0)
         late_lay6 = z_pairs[1][:, 0].rearrange("p u c e -> p (u c e)").bitcast(F32)[:, first]
-        cap(late_lay6, last - 1, limit[last - 1][:, second], lifted[last - 1][:, second])
-        money(last - 1, late_lay6, HALF, PICKS)
-        quarters = [slice(q * P, (q + 1) * P) for q in range(2)]
+        cap(late_lay6, 6, limit[6][:, second], lifted[6][:, second])
         late_lifted = z_il1[0][:].rearrange("p c t -> p (c t)").bitcast(F32)[:, first]
-        for q, cs in enumerate(quarters):
-            lift(late_lifted[:, cs], last, late_attach[:, cs], HALF + q * P, HALF + (q + 1) * P)
-        for cs in quarters:
-            cap(lay7[:, second][:, cs], last, late_limit[:, cs], late_lifted[:, cs])
-        for cs in quarters:
-            nc.vector.tensor_scalar(z_pairs[1][:, 1, 1, cs, 1], lay7[:, second][:, cs], term(2, last), None, ALU.mult)
-        store(0)
-        for cs in quarters:
-            weave(nc.vector.tensor_copy, z_il1[1][:, cs, :], 1, 1, cs)
-        for cs in quarters:
-            quantize(z_codes[1][:, second][:, cs], z_sc[1][:, second][:, cs], z_il1[1][:, cs, :])
+        quarters = [slice(0, P), slice(P, HALF)]
+        for cols in quarters:
+            lift(late_lifted[:, cols], 7, late_attach[:, cols], HALF + cols.start, HALF + cols.stop)
+        late_money(6, late_lay6, first)
+        for cols in quarters:
+            cap(lay7[:, second][:, cols], 7, late_limit[:, cols], late_lifted[:, cols])
+        for cols in quarters:
+            late_money(7, lay7[:, second][:, cols], cols)
+        store(0, (nc.scalar.copy, nc.scalar.copy))
+        for cols in quarters:
+            weave(nc.vector.tensor_copy, z_il1[1][:, cols, :], 1, 1, cols)
+        for cols in quarters:
+            quantize(z_codes[1][:, second][:, cols], z_sc[1][:, second][:, cols], z_il1[1][:, cols, :])
         second_product(1, 1)
-        store(1)
+        store(1, (nc.scalar.copy, nc.vector.tensor_copy))

@@ -21,8 +21,6 @@ P = 128
 PACK = 4
 PASS = P * PACK
 BANK = 512
-WINDOW = 2048
-WINDOWS = 4
 SLICES = H // P
 HALF = PICKS // 2
 EARLY = S + PASS
@@ -35,7 +33,6 @@ def tile_list_wildfire_layer_cession_kernel(
     nc = tc.nc
     with ExitStack() as ctx:
         held = ctx.enter_context(tc.tile_pool(name="held", bufs=1))
-        ring = ctx.enter_context(tc.tile_pool(name="ring", bufs=3))
         one = ctx.enter_context(tc.tile_pool(name="one", bufs=1))
         psum_h = ctx.enter_context(tc.psum_pool(name="psum_h", bufs=4))
         psum_o = ctx.enter_context(tc.psum_pool(name="psum_o", bufs=1))
@@ -75,6 +72,8 @@ def tile_list_wildfire_layer_cession_kernel(
             nc.vector.memset(raw[64:128, :], 0)
         planes_early = held.tile([P, 2, EARLY // 4], I32, name="planes_early", align_bytes=64)
         nc.gpsimd.memset(planes_early[:], 0)
+        unit = held.tile([P, 1], F32, name="unit")
+        nc.scalar.activation(unit[:], zero[:, 0:1], ACT.Exp)
 
         term_raw = held.tile([P, PASS], F32, name="term_raw")
         nc.gpsimd.memset(term_raw[:], 0.0)
@@ -83,21 +82,14 @@ def tile_list_wildfire_layer_cession_kernel(
         ident = held.tile([P, P], F32, name="ident")
         make_identity(nc, ident[:])
         term_rows = held.tile([P, PACK, P], F32, name="term_rows")
-        terms = held.tile([P, PACK, 6], F32, name="terms")
+        terms = held.tile([P, 6, PACK], F32, name="terms")
         ATT, LIM, GAIN = range(3)
 
-        def place(i):
-            return i // PACK, (2, 0, 1, 3)[i % PACK]
-
         def term(v, i):
-            b, t = place(i)
-            return terms[:, t, 2 * v + b : 2 * v + b + 1]
+            b, t = divmod(i, PACK)
+            return terms[:, 2 * v + b, t : t + 1]
 
-        windows = []
-        for w in range(WINDOWS):
-            win = held.tile([P, WINDOW], F32, name="win%d" % w, align_bytes=64)
-            nc.scalar.activation(win[:, S:WINDOW], zero[:, 0:1].to_broadcast([P, WINDOW - S]), ACT.Exp)
-            windows.append(win)
+        windows = [held.tile([P, S], F32, name="win%d" % w, align_bytes=64) for w in range(SLICES)]
 
         nc.scalar.copy(
             term_rows[:].rearrange("p t (g q) -> p t g q", q=8),
@@ -149,24 +141,15 @@ def tile_list_wildfire_layer_cession_kernel(
         move_rows(planes_late, slice(EARLY // 4, (S + H) // 4))
         for t in range(PACK):
             nc.sync.dma_start(out=ws_raw[:, 1, t, :], in_=ws_view[1, t])
-        ws_sc = [held.tile([P, N], U8, name="ws_sc%d" % b, align_bytes=64) for b in range(2)]
-        z_pairs = [held.tile([P, 2, 2, HALF, 2], BF16, name="z_pairs%d" % b, align_bytes=64) for b in range(2)]
-        z_il0 = held.tile([P, PICKS, PACK], BF16, name="z_il0", align_bytes=64)
         z_codes = [held.tile([P, PICKS], U32, name="z_codes%d" % b, align_bytes=64) for b in range(2)]
         z_sc = [held.tile([P, PICKS], U8, name="z_sc%d" % b, align_bytes=64) for b in range(2)]
-
-        def weave(copy, dst, b, half, cols):
-            pairs = z_pairs[b][:, half].rearrange("p u c e -> p u (c e)").bitcast(U32)
-            copy(
-                dst.rearrange("p c t -> p (c t)").bitcast(U32).rearrange("p (c u) -> p c u", u=2),
-                pairs[:, :, cols].rearrange("p u c -> p c u"),
-            )
+        layered = [held.tile([P, 2, PACK, HALF], F32, name="layered%d" % b) for b in range(2)]
 
         def quantize(codes, scales, il):
             nc.vector.quantize_mx(out=codes.bitcast(FP8X4), scales=scales, in_=il.rearrange("p n t -> p (n t)"))
 
         def h_pass(i, a, dst, c0, c1):
-            b, t = place(i)
+            b, t = divmod(i, PACK)
             if b == 0:
                 w4_plane = planes_early[:, a, :].bitcast(U8)[:, S + P * t : S + P * (t + 1)]
             else:
@@ -186,7 +169,7 @@ def tile_list_wildfire_layer_cession_kernel(
                 bank = psum_h.tile([P, BANK], F32, name="h_bank")
                 for a in range(2):
                     h_pass(i, a, bank[:], half * BANK, (half + 1) * BANK)
-                nc.scalar.copy(windows[i % WINDOWS][:, half * BANK : (half + 1) * BANK], bank[:])
+                nc.scalar.copy(windows[i][:, half * BANK : (half + 1) * BANK], bank[:])
 
         def first_slice():
             banks = [psum_h.tile([P, BANK], F32, name="h_bank")]
@@ -200,29 +183,55 @@ def tile_list_wildfire_layer_cession_kernel(
                 copy = (nc.vector.tensor_copy, nc.scalar.copy)[j % 2]
                 copy(windows[0][:, BANK + j * P : BANK + (j + 1) * P], banks[1 + j][:])
 
-        loss = {}
+        loss, attach, limit, lifted = {}, {}, {}, {}
+        for i in range(SLICES):
+            loss[i] = one.tile([P, PICKS], F32, name="loss%d" % i, tag="loss%d" % i, align_bytes=64)
+            attach[i] = one.tile([P, PICKS], F32, name="attach%d" % i, tag="attach%d" % i, align_bytes=64)
+            limit[i] = one.tile([P, PICKS], F32, name="limit%d" % i, tag="limit%d" % i, align_bytes=64)
+        lift_bufs = [held.tile([P, PICKS], F32, name="lift_buf%d" % n) for n in range(2)]
+        whole, first, second = slice(0, PICKS), slice(0, HALF), slice(HALF, PICKS)
 
-        def pick_loss(i):
-            loss[i] = ring.tile([P, PICKS], F32, name="loss", bufs=4)
-            nc.scalar.activation(loss[i][:], windows[i % WINDOWS][:].indirect(pos1_t[:]), ACT.Exp)
+        def picked(i, pos_t, cols):
+            return windows[i][:].indirect(pos_t[:, cols.start // 16 : cols.stop // 16])
 
-        def pick(dst, i, pos_t, c0, c1):
-            nc.vector.tensor_copy(dst, windows[i % WINDOWS][:, 0:S].indirect(pos_t[:, c0 // 16 : c1 // 16]))
+        def pick_loss(i, cols=whole):
+            nc.scalar.activation(loss[i][:, cols], picked(i, pos1_t, cols), ACT.Exp, scale=unit[:])
 
-        def lift(dst, i, picked, c0, c1):
-            nc.vector.scalar_tensor_tensor(dst, picked, term(ATT, i), loss[i][:, c0:c1], ALU.add, ALU.max)
+        def on_vector(dst, src):
+            nc.vector.tensor_copy(dst, src)
 
-        def cap(dst, i, picked, lifted_loss):
-            nc.vector.scalar_tensor_tensor(dst, picked, term(LIM, i), lifted_loss, ALU.add, ALU.min)
+        def on_scalar(dst, src):
+            nc.scalar.activation(dst, src, ACT.Copy)
 
-        def money(i, src, c0, c1):
-            b, t = place(i)
-            dst = z_pairs[b][:, c0 // HALF : c1 // HALF, t // 2, :, t % 2]
-            nc.scalar.activation(dst, src.rearrange("p (h c) -> p h c", c=HALF), ACT.Copy, scale=term(GAIN, i))
+        def pick_attach(i, engine, cols=whole):
+            engine(attach[i][:, cols], picked(i, pos2_t, cols))
 
-        def late_money(i, src, cols):
-            b, t = place(i)
-            nc.vector.tensor_scalar(z_pairs[b][:, 1, t // 2, cols, t % 2], src, term(GAIN, i), None, ALU.mult)
+        def pick_limit(i, engine, cols=whole):
+            engine(limit[i][:, cols], picked(i, pos3_t, cols))
+
+        def lift(i, cols=whole):
+            nc.vector.scalar_tensor_tensor(
+                lift_bufs[i % 2][:, cols], attach[i][:, cols], term(ATT, i), loss[i][:, cols], ALU.add, ALU.max
+            )
+
+        def cap(i, halves=slice(0, 2), cols=slice(0, HALF)):
+            b, t = divmod(i, PACK)
+
+            def by_half(tile):
+                return tile[:].rearrange("p (h c) -> p h c", h=2)[:, halves, cols]
+
+            nc.vector.scalar_tensor_tensor(
+                layered[b][:, halves, t, cols], by_half(limit[i]), term(LIM, i), by_half(lift_bufs[i % 2]), ALU.add, ALU.min
+            )
+
+        def money(dst, b, half, cols):
+            n = cols.stop - cols.start
+            nc.vector.tensor_tensor(
+                dst.rearrange("p (c x) t -> p c t x", x=2),
+                layered[b][:, half, :, cols].rearrange("p t (c x) -> p c t x", x=2),
+                terms[:, 2 * GAIN + b, :].rearrange("p (c t x) -> p c t x", c=1, x=1).to_broadcast([P, n // 2, PACK, 2]),
+                ALU.mult,
+            )
 
         acc = {}
         ws_block = {}
@@ -233,10 +242,11 @@ def tile_list_wildfire_layer_cession_kernel(
                     acc[j, half] = psum_o.tile([P, HALF], F32, name="acc%d%d" % (j, half))
                 elif b == 0:
                     acc[j, half] = psum_h.tile([P, BANK], F32, name="h_bank")
+                codes, scales = ws_block[b, j]
                 nc.tensor.matmul_mx(
                     out=acc[j, half][:, 0:HALF],
-                    lhsT=ws_block[b, j].bitcast(FP8X4),
-                    lhsT_scale=ws_sc[b][:, j * P : (j + 1) * P],
+                    lhsT=codes.bitcast(FP8X4),
+                    lhsT_scale=scales,
                     rhs=z_codes[b][:, half * HALF : (half + 1) * HALF].bitcast(FP8X4),
                     rhs_scale=z_sc[b][:, half * HALF : (half + 1) * HALF],
                     start=(b == 0),
@@ -256,28 +266,27 @@ def tile_list_wildfire_layer_cession_kernel(
 
         ws_il = {}
 
-        def ws_rows(piece, cols):
-            b, s = divmod(piece, 2)
-            return ws_raw[:, b, :, s * HALF : (s + 1) * HALF][:, :, cols]
+        def round_on_gpsimd(dst, src):
+            nc.gpsimd.tensor_scalar(dst, src.rearrange("p t n -> p n t"), 1.0, 0.0, ALU.mult, ALU.add)
 
-        def round_ws(piece, tag, cols):
-            ws_il[piece] = one.tile([P, HALF, PACK], BF16, name="ws_il%d" % piece, tag=tag, align_bytes=64)
-            src = ws_rows(piece, cols).rearrange("p t n -> p n t")
-            nc.gpsimd.tensor_scalar(ws_il[piece][:, cols, :], src, 1.0, 0.0, ALU.mult, ALU.add)
+        def round_on_vector(dst, src):
+            nc.vector.tensor_copy(dst.rearrange("p (c x) t -> p c t x", x=2), src.rearrange("p t (c x) -> p c t x", x=2))
 
-        def round_ws_on_scalar(piece, cols):
-            nc.scalar.copy(
-                ws_il[piece][:, cols, :].rearrange("p (c x) t -> p c t x", x=4),
-                ws_rows(piece, cols).rearrange("p t (c x) -> p c t x", x=4),
-            )
+        def round_ws(engine, k0, k1, tag):
+            ws_il[k0] = one.tile([P, (k1 - k0) * P, PACK], BF16, name="ws_il%d" % k0, tag=tag, align_bytes=64)
+            for b in range(2):
+                lo, hi = max(k0, PACK * b), min(k1, PACK * (b + 1))
+                if lo < hi:
+                    src = ws_raw[:, b, :, (lo - PACK * b) * P : (hi - PACK * b) * P]
+                    engine(ws_il[k0][:, (lo - k0) * P : (hi - k0) * P, :], src)
 
-        def quantize_ws(pieces, tag):
-            codes = one.tile([P, len(pieces), HALF], U32, name="ws_codes%d" % pieces[0], tag=tag, align_bytes=64)
-            for n, piece in enumerate(pieces):
-                b, s = divmod(piece, 2)
-                quantize(codes[:, n, :], ws_sc[b][:, s * HALF : (s + 1) * HALF], ws_il[piece][:])
-                for u in range(2):
-                    ws_block[b, 2 * s + u] = codes[:, n, u * P : (u + 1) * P]
+        def quantize_ws(k0, k1, tag):
+            codes = one.tile([P, (k1 - k0) * P], U32, name="ws_codes%d" % k0, tag=tag, align_bytes=64)
+            scales = held.tile([P, (k1 - k0) * P], U8, name="ws_sc%d" % k0, align_bytes=64)
+            quantize(codes[:], scales[:], ws_il[k0][:])
+            for k in range(k0, k1):
+                cols = slice((k - k0) * P, (k - k0 + 1) * P)
+                ws_block[divmod(k, PACK)] = (codes[:, cols], scales[:, cols])
 
         warm = psum_o.tile([P, BANK], F32, name="acc20")
         for turn in range(4):
@@ -295,143 +304,84 @@ def tile_list_wildfire_layer_cession_kernel(
         turned = psum_h.tile([P, BANK], F32, name="h_bank")
         for t in range(PACK):
             nc.tensor.transpose(turned[:, t * P : (t + 1) * P], term_rows[:, t, :], ident[:])
-        nc.scalar.copy(terms[:], turned[:].rearrange("p (t j) -> p t j", t=PACK)[:, :, 0:6])
+        nc.scalar.copy(terms[:], turned[:].rearrange("p (t j) -> p j t", t=PACK)[:, 0:6, :])
 
-        attach, limit, excess, lifted, layered = {}, {}, {}, {}, {}
-        last = SLICES - 1
-        first, second = slice(0, HALF), slice(HALF, PICKS)
 
-        def width(i):
-            return HALF if i == last else PICKS
-
-        def pick_attach(i):
-            attach[i] = one.tile([P, PICKS], F32, name="attach%d" % i, tag="attach%d" % i, align_bytes=64)
-            pick(attach[i][:, 0 : width(i)], i, pos2_t, 0, width(i))
-
-        def pick_limit(i):
-            limit[i] = one.tile([P, PICKS], F32, name="limit%d" % i, tag="limit%d" % i, align_bytes=64)
-            pick(limit[i][:, 0 : width(i)], i, pos3_t, 0, width(i))
-
-        lift_bufs = [held.tile([P, PICKS], F32, name="lift_buf%d" % n) for n in range(3)]
-        lay_bufs = [held.tile([P, PICKS], F32, name="lay_buf%d" % n) for n in range(2)]
-
-        def lift_slice(i):
-            lifted[i] = lift_bufs[2 if i % 2 else i // 2 % 2]
-            lift(lifted[i][:, 0 : width(i)], i, attach[i][:, 0 : width(i)], 0, width(i))
-
-        def pick_excess(i):
-            excess[i] = ring.tile([P, PICKS], F32, name="excess", bufs=2)
-            nc.vector.tensor_tensor(excess[i][:], windows[i % WINDOWS][:].indirect(pos2_t[:]), loss[i][:], ALU.subtract)
-
-        def lift_by_excess(i):
-            rise = ring.tile([P, PICKS], F32, name="rise", bufs=2)
-            nc.scalar.activation(rise[:], excess[i][:], ACT.Relu, bias=term(ATT, i))
-            lifted[i] = lift_bufs[i // 2 % 2]
-            nc.gpsimd.tensor_tensor(lifted[i][:], loss[i][:], rise[:], ALU.add)
-
-        def cap_slice(i):
-            layered[i] = lay_bufs[i % 2][:, :]
-            cap(layered[i], i, limit[i][:], lifted[i][:])
-
-        def money_slice(i):
-            money(i, layered[i], 0, PICKS)
-
-        def next_pair(even):
-            first_product(even + 2)
-            first_product(even + 3)
-
-        round_ws(0, "ws_il0", first)
-        pick_attach(0)
-        pick_limit(0)
-        pick_limit(1)
-        pick_loss(1)
+        round_ws(round_on_gpsimd, 0, 3, "ws_il0")
+        pick_attach(0, on_vector)
+        pick_limit(0, on_vector)
+        pick_attach(1, on_vector)
+        pick_limit(1, on_vector)
         pick_loss(0)
-        pick_excess(1)
-        lift_slice(0)
-        cap_slice(0)
-        round_ws(1, "limit0", slice(0, P))
-        next_pair(0)
-        lift_by_excess(1)
+        pick_loss(1)
+        lift(0)
+        lift(1)
+        cap(0)
+        cap(1)
+        round_ws(round_on_gpsimd, 3, 5, "limit1")
+        first_product(2)
+        first_product(3)
 
-        pick_attach(2)
-        pick_limit(2)
-        pick_limit(3)
+        pick_attach(2, on_vector)
+        pick_limit(2, on_vector)
+        pick_attach(3, on_vector)
         pick_loss(2)
         pick_loss(3)
-        lift_slice(2)
-        pick_excess(3)
-        quantize_ws((0,), "attach2")
-        cap_slice(1)
-        money_slice(0)
-        cap_slice(2)
-        round_ws(2, "limit2", first)
-        round_ws_on_scalar(1, slice(P, HALF))
-        next_pair(2)
-        lift_by_excess(3)
+        pick_limit(3, on_scalar)
+        lift(2)
+        lift(3)
+        quantize_ws(0, 3, "attach2")
+        cap(2)
+        cap(3)
+        round_ws(round_on_gpsimd, 5, 6, "limit3")
+        first_product(4)
+        first_product(5)
 
-        pick_attach(4)
-        pick_limit(4)
-        pick_attach(5)
-        pick_limit(5)
+        pick_attach(4, on_vector)
+        pick_attach(5, on_vector)
         pick_loss(4)
         pick_loss(5)
-        lift_slice(4)
-        lift_slice(5)
-        quantize_ws((1,), "attach4")
-        money_slice(1)
-        cap_slice(3)
-        money_slice(2)
-        cap_slice(4)
-        round_ws(3, "limit4", first)
-        next_pair(4)
+        pick_limit(4, on_scalar)
+        pick_limit(5, on_scalar)
+        lift(4)
+        lift(5)
+        z_il0 = one.tile([P, PICKS, PACK], BF16, name="z_il0", tag="attach4", align_bytes=64)
+        for half, cols in enumerate((first, second)):
+            money(z_il0[:, cols, :], 0, half, first)
+        quantize_ws(3, 5, "attach5")
+        cap(4)
+        cap(5)
+        quantize(z_codes[0][:], z_sc[0][:], z_il0[:])
+        round_ws(round_on_vector, 6, 8, "attach4")
+        quantize_ws(5, 6, "limit5")
+        first_product(6)
+        first_product(7)
 
-        pick_attach(6)
-        pick_limit(6)
-        pick_attach(7)
-        pick_limit(7)
         pick_loss(6)
-        lift_slice(6)
-        quantize_ws((2, 3), "attach6")
-        money_slice(3)
-        money_slice(4)
-        cap_slice(5)
-        pick_loss(7)
-        weave(nc.scalar.copy, z_il0[:, first, :], 0, 0, first)
-        weave(nc.scalar.copy, z_il0[:, second, :], 0, 1, first)
-        money_slice(5)
-        lift_slice(7)
-        quantize(z_codes[0][:, first], z_sc[0][:, first], z_il0[:, first, :])
+        pick_attach(6, on_scalar)
+        pick_limit(6, on_scalar)
+        for cols in (first, second):
+            pick_loss(7, cols)
+            pick_attach(7, on_scalar, cols)
+            pick_limit(7, on_scalar, cols)
+        lift(6)
+        quantize_ws(6, 8, "wsc6")
+        cap(6)
         second_product(0, 0)
-        lay6 = windows[7 % WINDOWS][:, S : S + HALF]
-        lay7 = lay_bufs[0]
-        cap(lay6, 6, limit[6][:, first], lifted[6][:, first])
-        cap(lay7[:, first], 7, limit[7][:, first], lifted[7][:, first])
-        quantize(z_codes[0][:, second], z_sc[0][:, second], z_il0[:, second, :])
         second_product(0, 1)
-        money(6, lay6, 0, HALF)
-        money(7, lay7[:, first], 0, HALF)
         z_il1 = [held.tile([P, HALF, PACK], BF16, name="z_il1%d" % half, align_bytes=64) for half in range(2)]
-        weave(nc.scalar.copy, z_il1[0][:], 1, 0, first)
-
-        late_attach, late_limit = limit[6][:, first], limit[7][:, first]
-        pick(late_attach, 7, pos2_t, HALF, PICKS)
-        pick(late_limit, 7, pos3_t, HALF, PICKS)
+        lift(7, first)
+        cap(7, slice(0, 1))
+        money(z_il1[0][:], 1, 0, first)
+        lift(7, second)
         quantize(z_codes[1][:, first], z_sc[1][:, first], z_il1[0][:])
         second_product(1, 0)
-        late_lay6 = z_pairs[1][:, 0].rearrange("p u c e -> p (u c e)").bitcast(F32)[:, first]
-        cap(late_lay6, 6, limit[6][:, second], lifted[6][:, second])
-        late_lifted = z_il1[0][:].rearrange("p c t -> p (c t)").bitcast(F32)[:, first]
         quarters = [slice(0, P), slice(P, HALF)]
         for cols in quarters:
-            lift(late_lifted[:, cols], 7, late_attach[:, cols], HALF + cols.start, HALF + cols.stop)
-        late_money(6, late_lay6, first)
+            cap(7, slice(1, 2), cols)
         for cols in quarters:
-            cap(lay7[:, second][:, cols], 7, late_limit[:, cols], late_lifted[:, cols])
-        for cols in quarters:
-            late_money(7, lay7[:, second][:, cols], cols)
+            money(z_il1[1][:, cols, :], 1, 1, cols)
         store(0, (nc.scalar.copy, nc.scalar.copy))
-        for cols in quarters:
-            weave(nc.vector.tensor_copy, z_il1[1][:, cols, :], 1, 1, cols)
         for cols in quarters:
             quantize(z_codes[1][:, second][:, cols], z_sc[1][:, second][:, cols], z_il1[1][:, cols, :])
         second_product(1, 1)

from contextlib import ExitStack

import concourse.mybir as mybir
from concourse.masks import make_identity

T, S, PICKS, K, H, N = 4096, 1024, 512, 1024, 1024, 512
FLOPS = 2 * K * H * S + 2 * H * N * PICKS

F32 = mybir.dt.float32
BF16 = mybir.dt.bfloat16
I32 = mybir.dt.int32
U32 = mybir.dt.uint32
U16 = mybir.dt.uint16
U8 = mybir.dt.uint8
FP8X4 = mybir.dt.float8_e4m3fn_x4
FP4X4 = mybir.dt.float4_e2m1fn_x4
ALU = mybir.AluOpType
ACT = mybir.ActivationFunctionType

P = 128
PACK = 4
PASS = P * PACK
BANK = 512
SLICES = H // P
HALF = PICKS // 2
EARLY = S + PASS
QUADRANTS = (0, 2, 1, 3)


def tile_list_wildfire_layer_cession_kernel(
    tc, tab_words, tab_scales, offs, pos1, pos2, pos3, w4_words, w4_scales, att, lim, gain, ws, out
):
    nc = tc.nc
    with ExitStack() as ctx:
        held = ctx.enter_context(tc.tile_pool(name="held", bufs=1))
        one = ctx.enter_context(tc.tile_pool(name="one", bufs=1))
        psum_h = ctx.enter_context(tc.psum_pool(name="psum_h", bufs=4))
        psum_o = ctx.enter_context(tc.psum_pool(name="psum_o", bufs=1))

        offs_t = held.tile([P, S // 16], U16, name="offs_t")
        pos1_t = held.tile([P, PICKS // 16], U16, name="pos1_t")
        pos2_t = held.tile([P, PICKS // 16], U16, name="pos2_t")
        pos3_t = held.tile([P, PICKS // 16], U16, name="pos3_t")

        w4_sc_raw = held.tile([P, H // 4], I32, name="w4_sc_raw", align_bytes=64)
        tab_sc = held.tile([P, T // 4], I32, name="tab_sc", align_bytes=64)
        w4_view = w4_words.rearrange("a p n -> p a n").bitcast(I32)
        w4_raw0 = held.tile([P, 2, H // 4], I32, name="w4_raw0", align_bytes=64)
        tab_w = [one.tile([P, T], I32, name="tab_w%d" % a, tag="big%d" % a, align_bytes=64) for a in range(2)]

        def load_scales(raw, scales):
            for a in range(2):
                nc.sync.dma_start(out=raw[a:32:2, :], in_=scales[a].bitcast(I32))

        def load_table(a):
            nc.sync.dma_start(out=tab_w[a][:], in_=tab_words[a].rearrange("p t i -> p (t i)").bitcast(I32))

        nc.sync.dma_start(out=w4_raw0[:], in_=w4_view[:, :, 0 : H // 4])
        load_scales(tab_sc, tab_scales)
        nc.sync.dma_start(offs_t[:], offs)
        load_table(0)
        load_scales(w4_sc_raw, w4_scales)
        nc.sync.dma_start(pos1_t[:], pos1)
        load_table(1)
        nc.sync.dma_start(pos2_t[:], pos2)
        nc.sync.dma_start(pos3_t[:], pos3)

        zero = held.tile([P, 8], F32, name="zero")
        nc.vector.memset(zero[:], 0.0)
        for raw in (w4_sc_raw, tab_sc):
            nc.vector.memset(raw[32:64, :], 0)
            nc.vector.memset(raw[64:128, :], 0)
        planes_early = held.tile([P, 2, EARLY // 4], I32, name="planes_early", align_bytes=64)
        nc.gpsimd.memset(planes_early[:], 0)
        unit = held.tile([P, 1], F32, name="unit")
        nc.scalar.activation(unit[:], zero[:, 0:1], ACT.Exp)

        term_raw = held.tile([P, PASS], F32, name="term_raw")
        nc.gpsimd.memset(term_raw[:], 0.0)
        for v, vec in enumerate((att, lim, gain)):
            nc.gpsimd.dma_start(out=term_raw[2 * v : 2 * v + 2, :], in_=vec.rearrange("(b k) -> b k", b=2))
        ident = held.tile([P, P], F32, name="ident")
        make_identity(nc, ident[:])
        term_rows = held.tile([P, PACK, P], F32, name="term_rows")
        terms = held.tile([P, 6, PACK], F32, name="terms")
        ATT, LIM, GAIN = range(3)

        def term(v, i):
            b, t = divmod(i, PACK)
            return terms[:, 2 * v + b, t : t + 1]

        windows = [held.tile([P, S], F32, name="win%d" % w, align_bytes=64) for w in range(SLICES)]

        nc.scalar.copy(
            term_rows[:].rearrange("p t (g q) -> p t g q", q=8),
            term_raw[:].rearrange("p (g t q) -> p t g q", t=PACK, q=8),
        )

        rows = held.tile([P, (S + H) // 4], I32, name="rows", align_bytes=64)
        nc.vector.tensor_copy(
            out=rows[:, S // 4 :].rearrange("p (b t g x) -> p b t g x", b=2, t=PACK, x=2),
            in_=w4_sc_raw[:].rearrange("p (b g t x) -> p b t g x", b=2, t=PACK, x=2),
        )
        v_sc_rows = one.tile([P, S], U8, name="v_sc_rows", tag="late", align_bytes=64)
        nc.vector.tensor_copy(v_sc_rows[:], tab_sc[:].bitcast(U8).indirect(offs_t[:]))
        w4_codes = [held.tile([P, 2, H // 4], I32, name="w4_codes%d" % b, align_bytes=64) for b in range(2)]

        def order_columns(b, raw):
            nc.vector.tensor_copy(
                out=w4_codes[b][:].rearrange("p a (t g x) -> p a t g x", t=PACK, x=4),
                in_=raw[:].rearrange("p a (g t x) -> p a t g x", t=PACK, x=4),
            )

        def move_rows(planes, words):
            for quad in QUADRANTS:
                nc.sync.dma_start(out=planes[32 * quad : 32 * quad + 4, :, :], in_=rows[8 * quad : 8 * quad + 8, words])

        nc.vector.tensor_copy(rows[:, 0 : S // 4], v_sc_rows[:].bitcast(I32))
        move_rows(planes_early, slice(0, EARLY // 4))
        w4_raw1 = one.tile([P, 2, H // 4], I32, name="w4_raw1", tag="late", align_bytes=64)
        nc.sync.dma_start(out=w4_raw1[:], in_=w4_view[:, :, H // 4 : H // 2])
        order_columns(0, w4_raw0)

        v_codes = []
        for a in range(2):
            codes = held.tile([P, S], U32, name="v_codes%d" % a, align_bytes=64)
            for half in range(2):
                nc.vector.tensor_copy(
                    codes[:, half * BANK : (half + 1) * BANK],
                    tab_w[a][:].bitcast(U32).indirect(offs_t[:, half * BANK // 16 : (half + 1) * BANK // 16]),
                )
            v_codes.append(codes)
        order_columns(1, w4_raw1)

        ws_raw = one.tile([P, 2, PACK, N], F32, name="ws_raw", tag="big0", align_bytes=64)
        ws_view = ws.rearrange("(b g t q) n -> b t g q n", b=2, t=PACK, q=8)
        for t in range(PACK):
            nc.sync.dma_start(out=ws_raw[:, 0, t, :], in_=ws_view[0, t])
        planes_late = one.tile([P, 2, PASS // 4], I32, name="planes_late", tag="big1", align_bytes=64)
        nc.gpsimd.memset(planes_late[:], 0)
        move_rows(planes_late, slice(EARLY // 4, (S + H) // 4))
        for t in range(PACK):
            nc.sync.dma_start(out=ws_raw[:, 1, t, :], in_=ws_view[1, t])
        z_codes = [held.tile([P, PICKS], U32, name="z_codes%d" % b, align_bytes=64) for b in range(2)]
        z_sc = [held.tile([P, PICKS], U8, name="z_sc%d" % b, align_bytes=64) for b in range(2)]
        layered = [held.tile([P, 2, PACK, HALF], F32, name="layered%d" % b) for b in range(2)]

        def quantize(codes, scales, il):
            nc.vector.quantize_mx(out=codes.bitcast(FP8X4), scales=scales, in_=il.rearrange("p n t -> p (n t)"))

        def h_pass(i, a, dst, c0, c1):
            b, t = divmod(i, PACK)
            if b == 0:
                w4_plane = planes_early[:, a, :].bitcast(U8)[:, S + P * t : S + P * (t + 1)]
            else:
                w4_plane = planes_late[:, a, :].bitcast(U8)[:, P * t : P * (t + 1)]
            nc.tensor.matmul_mx(
                out=dst,
                lhsT=w4_codes[b][:, a, :].bitcast(U8)[:, 2 * P * t : 2 * P * (t + 1)].bitcast(FP4X4),
                lhsT_scale=w4_plane,
                rhs=v_codes[a][:, c0:c1].bitcast(FP8X4),
                rhs_scale=planes_early[:, a, :].bitcast(U8)[:, c0:c1],
                start=(a == 0),
                stop=(a == 1),
            )

        def first_product(i):
            for half in range(2):
                bank = psum_h.tile([P, BANK], F32, name="h_bank")
                for a in range(2):
                    h_pass(i, a, bank[:], half * BANK, (half + 1) * BANK)
                nc.scalar.copy(windows[i][:, half * BANK : (half + 1) * BANK], bank[:])

        def first_slice():
            banks = [psum_h.tile([P, BANK], F32, name="h_bank")]
            banks += [psum_o.tile([P, P], F32, name="acc%d0" % j) for j in range(4)]
            for a in range(2):
                h_pass(0, a, banks[0][:], 0, BANK)
                for j in range(4):
                    h_pass(0, a, banks[1 + j][:], BANK + j * P, BANK + (j + 1) * P)
            nc.scalar.copy(windows[0][:, 0:BANK], banks[0][:])
            for j in range(4):
                copy = (nc.vector.tensor_copy, nc.scalar.copy)[j % 2]
                copy(windows[0][:, BANK + j * P : BANK + (j + 1) * P], banks[1 + j][:])

        loss, attach, limit, lifted = {}, {}, {}, {}
        for i in range(SLICES):
            loss[i] = one.tile([P, PICKS], F32, name="loss%d" % i, tag="loss%d" % i, align_bytes=64)
            attach[i] = one.tile([P, PICKS], F32, name="attach%d" % i, tag="attach%d" % i, align_bytes=64)
            limit[i] = one.tile([P, PICKS], F32, name="limit%d" % i, tag="limit%d" % i, align_bytes=64)
        lift_bufs = [held.tile([P, PICKS], F32, name="lift_buf%d" % n) for n in range(2)]
        whole, first, second = slice(0, PICKS), slice(0, HALF), slice(HALF, PICKS)

        def picked(i, pos_t, cols):
            return windows[i][:].indirect(pos_t[:, cols.start // 16 : cols.stop // 16])

        def pick_loss(i, cols=whole):
            nc.scalar.activation(loss[i][:, cols], picked(i, pos1_t, cols), ACT.Exp, scale=unit[:])

        def on_vector(dst, src):
            nc.vector.tensor_copy(dst, src)

        def on_scalar(dst, src):
            nc.scalar.activation(dst, src, ACT.Copy)

        def pick_attach(i, engine, cols=whole):
            engine(attach[i][:, cols], picked(i, pos2_t, cols))

        def pick_limit(i, engine, cols=whole):
            engine(limit[i][:, cols], picked(i, pos3_t, cols))

        def lift(i, cols=whole):
            nc.vector.scalar_tensor_tensor(
                lift_bufs[i % 2][:, cols], attach[i][:, cols], term(ATT, i), loss[i][:, cols], ALU.add, ALU.max
            )

        def cap(i, halves=slice(0, 2), cols=slice(0, HALF)):
            b, t = divmod(i, PACK)

            def by_half(tile):
                return tile[:].rearrange("p (h c) -> p h c", h=2)[:, halves, cols]

            nc.vector.scalar_tensor_tensor(
                layered[b][:, halves, t, cols], by_half(limit[i]), term(LIM, i), by_half(lift_bufs[i % 2]), ALU.add, ALU.min
            )

        def money(dst, b, half, cols):
            n = cols.stop - cols.start
            nc.vector.tensor_tensor(
                dst.rearrange("p (c x) t -> p c t x", x=2),
                layered[b][:, half, :, cols].rearrange("p t (c x) -> p c t x", x=2),
                terms[:, 2 * GAIN + b, :].rearrange("p (c t x) -> p c t x", c=1, x=1).to_broadcast([P, n // 2, PACK, 2]),
                ALU.mult,
            )

        acc = {}
        ws_block = {}

        def second_product(b, half):
            for j in range(N // P):
                if b == 0 and half == 0:
                    acc[j, half] = psum_o.tile([P, HALF], F32, name="acc%d%d" % (j, half))
                elif b == 0:
                    acc[j, half] = psum_h.tile([P, BANK], F32, name="h_bank")
                codes, scales = ws_block[b, j]
                nc.tensor.matmul_mx(
                    out=acc[j, half][:, 0:HALF],
                    lhsT=codes.bitcast(FP8X4),
                    lhsT_scale=scales,
                    rhs=z_codes[b][:, half * HALF : (half + 1) * HALF].bitcast(FP8X4),
                    rhs_scale=z_sc[b][:, half * HALF : (half + 1) * HALF],
                    start=(b == 0),
                    stop=(b == 1),
                )

        out_view = out.rearrange("(j p) m -> p j m", p=P)

        def store(half, copies):
            for pair in range(2):
                res = held.tile([P, 2, HALF], F32, name="res%d%d" % (pair, half))
                for u, copy in enumerate(copies):
                    copy(res[:, u, :], acc[2 * pair + u, half][:, 0:HALF])
                nc.sync.dma_start(
                    out=out_view[:, 2 * pair : 2 * pair + 2, half * HALF : (half + 1) * HALF], in_=res[:]
                )

        ws_il = {}

        def round_on_gpsimd(dst, src):
            nc.gpsimd.tensor_scalar(dst, src.rearrange("p t n -> p n t"), 1.0, 0.0, ALU.mult, ALU.add)

        def round_on_vector(dst, src):
            nc.vector.tensor_copy(dst.rearrange("p (c x) t -> p c t x", x=2), src.rearrange("p t (c x) -> p c t x", x=2))

        def round_ws(engine, k0, k1, tag):
            ws_il[k0] = one.tile([P, (k1 - k0) * P, PACK], BF16, name="ws_il%d" % k0, tag=tag, align_bytes=64)
            for b in range(2):
                lo, hi = max(k0, PACK * b), min(k1, PACK * (b + 1))
                if lo < hi:
                    src = ws_raw[:, b, :, (lo - PACK * b) * P : (hi - PACK * b) * P]
                    engine(ws_il[k0][:, (lo - k0) * P : (hi - k0) * P, :], src)

        def quantize_ws(k0, k1, tag):
            codes = one.tile([P, (k1 - k0) * P], U32, name="ws_codes%d" % k0, tag=tag, align_bytes=64)
            scales = held.tile([P, (k1 - k0) * P], U8, name="ws_sc%d" % k0, align_bytes=64)
            quantize(codes[:], scales[:], ws_il[k0][:])
            for k in range(k0, k1):
                cols = slice((k - k0) * P, (k - k0 + 1) * P)
                ws_block[divmod(k, PACK)] = (codes[:, cols], scales[:, cols])

        warm = psum_o.tile([P, BANK], F32, name="acc20")
        for turn in range(4):
            nc.tensor.matmul_mx(
                out=warm[:],
                lhsT=w4_codes[0][:, 0, :].bitcast(U8)[:, 0 : 2 * P].bitcast(FP4X4),
                lhsT_scale=rows[:].bitcast(U8)[:, S : S + P],
                rhs=v_codes[0][:, BANK:S].bitcast(FP8X4),
                rhs_scale=rows[:].bitcast(U8)[:, BANK:S],
                start=True,
                stop=True,
            )
        first_slice()
        first_product(1)
        turned = psum_h.tile([P, BANK], F32, name="h_bank")
        for t in range(PACK):
            nc.tensor.transpose(turned[:, t * P : (t + 1) * P], term_rows[:, t, :], ident[:])
        nc.scalar.copy(terms[:], turned[:].rearrange("p (t j) -> p j t", t=PACK)[:, 0:6, :])


        round_ws(round_on_gpsimd, 0, 3, "ws_il0")
        pick_attach(0, on_vector)
        pick_limit(0, on_vector)
        pick_attach(1, on_vector)
        pick_limit(1, on_vector)
        pick_loss(0)
        pick_loss(1)
        lift(0)
        lift(1)
        cap(0)
        cap(1)
        round_ws(round_on_gpsimd, 3, 5, "limit1")
        first_product(2)
        first_product(3)

        pick_attach(2, on_vector)
        pick_limit(2, on_vector)
        pick_attach(3, on_vector)
        pick_loss(2)
        pick_loss(3)
        pick_limit(3, on_scalar)
        lift(2)
        lift(3)
        quantize_ws(0, 3, "attach2")
        cap(2)
        cap(3)
        round_ws(round_on_gpsimd, 5, 6, "limit3")
        first_product(4)
        first_product(5)

        pick_attach(4, on_vector)
        pick_attach(5, on_vector)
        pick_loss(4)
        pick_loss(5)
        pick_limit(4, on_scalar)
        pick_limit(5, on_scalar)
        lift(4)
        lift(5)
        z_il0 = one.tile([P, PICKS, PACK], BF16, name="z_il0", tag="attach4", align_bytes=64)
        for half, cols in enumerate((first, second)):
            money(z_il0[:, cols, :], 0, half, first)
        quantize_ws(3, 5, "attach5")
        cap(4)
        cap(5)
        quantize(z_codes[0][:], z_sc[0][:], z_il0[:])
        round_ws(round_on_vector, 6, 8, "attach4")
        quantize_ws(5, 6, "limit5")
        first_product(6)
        first_product(7)

        pick_loss(6)
        pick_attach(6, on_scalar)
        pick_limit(6, on_scalar)
        for cols in (first, second):
            pick_loss(7, cols)
            pick_attach(7, on_scalar, cols)
            pick_limit(7, on_scalar, cols)
        lift(6)
        quantize_ws(6, 8, "wsc6")
        cap(6)
        second_product(0, 0)
        second_product(0, 1)
        z_il1 = [held.tile([P, HALF, PACK], BF16, name="z_il1%d" % half, align_bytes=64) for half in range(2)]
        lift(7, first)
        cap(7, slice(0, 1))
        money(z_il1[0][:], 1, 0, first)
        lift(7, second)
        quantize(z_codes[1][:, first], z_sc[1][:, first], z_il1[0][:])
        second_product(1, 0)
        quarters = [slice(0, P), slice(P, HALF)]
        for cols in quarters:
            cap(7, slice(1, 2), cols)
        for cols in quarters:
            money(z_il1[1][:, cols, :], 1, 1, cols)
        store(0, (nc.scalar.copy, nc.scalar.copy))
        for cols in quarters:
            quantize(z_codes[1][:, second][:, cols], z_sc[1][:, second][:, cols], z_il1[1][:, cols, :])
        second_product(1, 1)
        store(1, (nc.scalar.copy, nc.vector.tensor_copy))
